import numpy as np
import ml_dtypes


def mxq(x, axis, fmt="e4m3"):
    dtype, down = {"e4m3": (ml_dtypes.float8_e4m3fn, 7), "e5m2": (ml_dtypes.float8_e5m2, 14)}[fmt]
    v = np.moveaxis(np.asarray(x, np.float32).astype(ml_dtypes.bfloat16).astype(np.float64), axis, -1)
    blocks = v.reshape(v.shape[:-1] + (-1, 32))
    amax = np.abs(blocks).max(-1, keepdims=True)
    byte = np.maximum(np.where(amax > 0, np.frexp(amax)[1] - 1 + 127, 0) - down, 1)
    scale = np.exp2(byte - 127.0)
    codes = (blocks / scale).astype(np.float32).astype(dtype).astype(np.float64)
    return np.moveaxis((codes * scale).reshape(v.shape), -1, axis)


WIDE = False


def mx_kscale(k):
    if not WIDE:
        return np.ones(k)
    levels = np.array([10, -10, 5, -5, 0])
    if k % 512:
        return np.exp2(np.random.permutation(np.resize(levels, k // 32))).repeat(32)
    a = np.empty((k // 512, 16))
    for p in range(k // 512):
        a[p, :8] = np.random.permutation(np.resize(levels, 8))
        for g in range(8):
            far = levels[np.abs(levels - a[p, g]) >= 10]
            a[p, g + 8] = far[np.random.randint(len(far))]
    return np.exp2(a.ravel()).repeat(32)


def f64(x):
    return np.asarray(x).astype(np.float64)


def striped(idx):
    return np.tile(idx.reshape(-1, 16).T, (8, 1)).astype(np.uint16)


def unstriped(offs):
    return offs[:16].T.reshape(-1).astype(np.int64)


E2M1 = np.array([0.0, 0.5, 1.0, 1.5, 2.0, 3.0, 4.0, 6.0, -0.0, -0.5, -1.0, -1.5, -2.0, -3.0, -4.0, -6.0])


def pack_weight(w, fmt):
    k, n = w.shape
    w = f64(np.asarray(w, np.float32).astype(ml_dtypes.bfloat16)).reshape(k // 32, 32, n)
    amax = np.abs(w).max(1)
    if fmt == "e4m3":
        byte = np.frexp(amax)[1] - 1 + 127 - 7
    else:
        mant, ex = np.frexp(amax / 6.0)
        byte = np.where(mant > 0.5, ex, ex - 1) + 127
    byte = np.clip(np.where(amax > 0, byte, 1), 1, 254)
    scaled = (w * np.exp2(127.0 - byte)[:, None, :]).reshape(k, n).astype(np.float32)
    by_word = np.ascontiguousarray(scaled.reshape(k // 512, 128, 4, n).transpose(0, 1, 3, 2))
    if fmt == "e4m3":
        words = by_word.astype(ml_dtypes.float8_e4m3fn).view(np.uint8)
    else:
        c = by_word.astype(ml_dtypes.float4_e2m1fn).view(np.uint8) & 0xF
        words = (c[..., 0::2] | (c[..., 1::2] << 4)).reshape(k // 512, 128, 2 * n)
    return np.ascontiguousarray(words), np.ascontiguousarray(byte.astype(np.uint8).reshape(k // 512, 16, n))


def unpack_weight(words, scales, fmt):
    g, _, n = scales.shape
    words = np.ascontiguousarray(words).reshape(g, 128, n, -1)
    if fmt == "e4m3":
        vals = words.view(ml_dtypes.float8_e4m3fn).astype(np.float64)
    else:
        nib = np.empty((g, 128, n, 4), np.uint8)
        nib[..., 0::2] = words & 0xF
        nib[..., 1::2] = words >> 4
        vals = E2M1[nib]
    vals = vals * np.repeat(np.exp2(scales.astype(np.float64) - 127.0), 8, axis=1)[..., None]
    return vals.transpose(0, 1, 3, 2).reshape(g * 512, n)


def silu(v):
    return v / (1.0 + np.exp(-np.maximum(v, -700.0)))


K, T, E, C, H, N = 512, 1280, 4, 256, 512, 128


def by_expert(wq, xq):
    return np.concatenate([wq[e].T @ xq[:, e * C:(e + 1) * C] for e in range(E)], axis=1)


def setup_inputs():
    n = np.random.standard_normal
    s = mx_kscale(K)[:, None]
    u = mx_kscale(H)
    w1 = [pack_weight(m, "e2m1") for m in n((E, K, H)) / np.sqrt(K) / s[None] * u[None, None, :]]
    w2 = [pack_weight(m, "e2m1") for m in n((E, H, N)) / np.sqrt(H) / u[None, :, None]]
    x = pack_weight(n((K, T)) * s, "e4m3")
    return {
        "x_words": x[0],
        "x_scales": x[1],
        "xr": n((N, T)).astype(np.float32),
        "w1_words": np.stack([m[0] for m in w1]),
        "w1_scales": np.stack([m[1] for m in w1]),
        "w2_words": np.stack([m[0] for m in w2]),
        "w2_scales": np.stack([m[1] for m in w2]),
        "gate": np.tile(np.random.uniform(0.2, 1.0, E * C), (N, 1)).astype(np.float32),
        "offs": striped(np.random.permutation(T)[:E * C]),
    }


def reference(x_words, x_scales, xr, w1_words, w1_scales, w2_words, w2_scales, gate, offs):
    idx = unstriped(offs)
    w1 = np.stack([unpack_weight(w1_words[e], w1_scales[e], "e2m1") for e in range(E)])
    w2 = np.stack([unpack_weight(w2_words[e], w2_scales[e], "e2m1") for e in range(E)])
    xq = unpack_weight(x_words, x_scales, "e4m3")[:, idx]
    h = silu(by_expert(w1, xq))
    y = by_expert(w2, mxq(h, 0, "e4m3"))
    out = f64(xr).copy()
    out[:, idx] += f64(gate) * y
    return out

@@ -1,0 +1,174 @@
+from contextlib import ExitStack
+
+import concourse.mybir as mybir
+from concourse.masks import make_identity
+
+K, T, E, C, H, N = 512, 1280, 4, 256, 512, 128
+FLOPS = 2 * E * C * (K * H + H * N)
+
+F32 = mybir.dt.float32
+BF16 = mybir.dt.bfloat16
+I32 = mybir.dt.int32
+U32 = mybir.dt.uint32
+U16 = mybir.dt.uint16
+U8 = mybir.dt.uint8
+FP8X4 = mybir.dt.float8_e4m3fn_x4
+FP4X4 = mybir.dt.float4_e2m1fn_x4
+SILU = mybir.ActivationFunctionType.Silu
+MULT = mybir.AluOpType.mult
+ADD = mybir.AluOpType.add
+
+P = 128
+B = 128
+MODES = "TTTT"
+SCAT = "dddd"
+PIECES = [512,512,256]
+
+
+def tile_moe_res_mlp_silu_kernel(
+    tc, x_words, x_scales, xr, w1_words, w1_scales, w2_words, w2_scales, gate, offs, out
+):
+    nc = tc.nc
+    with ExitStack() as ctx:
+        keep = ctx.enter_context(tc.tile_pool(name="keep", bufs=1))
+        psum = ctx.enter_context(tc.psum_pool(name="psum", bufs=1))
+
+        offsets = keep.tile([P, E * C // 16], U16, name="offsets")
+        xw = keep.tile([P, T], I32, name="xw", align_bytes=64)
+        xs = keep.tile([P, T], U8, name="xs", align_bytes=64)
+        w1w = keep.tile([P, E, 2 * H], U8, name="w1w", align_bytes=64)
+        w1s = keep.tile([P, E, H], U8, name="w1s", align_bytes=64)
+        w2w = keep.tile([P, E, 2 * N], U8, name="w2w", align_bytes=64)
+        w2s = keep.tile([P, E, N], U8, name="w2s", align_bytes=64)
+        gate_sb = keep.tile([P, E * C], F32, name="gate_sb")
+        resid = keep.tile([P, T], F32, name="resid")
+        window = keep.tile([P, T], F32, name="window")
+        warm = keep.tile([P, 8], F32, name="warm")
+
+        nc.vector.memset(w1s[:].rearrange("p e c -> p (e c)").bitcast(I32), 0)
+        nc.vector.memset(w2s[:].rearrange("p e c -> p (e c)").bitcast(I32), 0)
+        nc.vector.memset(warm[:], 0.0)
+        nc.vector.memset(window[:], 0.0)
+
+        nc.sync.dma_start(offsets[:], offs)
+        for q in range(4):
+            rows = x_scales[0, 4 * q : 4 * q + 4, :].bitcast(I32)
+            nc.sync.dma_start(xs[32 * q : 32 * q + 32, :].bitcast(I32), rows.unsqueeze(0).to_broadcast([8, 4, T // 4]))
+        nc.sync.dma_start(xw[:], x_words[0].rearrange("p t r -> p (t r)").bitcast(I32))
+        w1v = w1_words.rearrange("e o p c -> p (e o) c").bitcast(I32)
+        nc.sync.dma_start(w1w[:, 0:1, :].bitcast(I32), w1v[:, 0:1, :])
+        for q in range(4):
+            nc.sync.dma_start(
+                w1s[32 * q : 32 * q + 4, :, :].bitcast(I32),
+                w1_scales[:, 0, 4 * q : 4 * q + 4, :].rearrange("e j c -> j e c").bitcast(I32),
+            )
+        nc.sync.dma_start(w1w[:, 1:E, :].bitcast(I32), w1v[:, 1:E, :])
+        nc.sync.dma_start(w2w[:].bitcast(I32), w2_words.rearrange("e o p c -> p (e o) c").bitcast(I32))
+        for q in range(4):
+            nc.sync.dma_start(
+                w2s[32 * q : 32 * q + 4, :, :].bitcast(I32),
+                w2_scales[:, 0, 4 * q : 4 * q + 4, :].rearrange("e j c -> j e c").bitcast(I32),
+            )
+        nc.sync.dma_start(gate_sb[:], gate)
+        nc.sync.dma_start(resid[:], xr)
+
+        nc.scalar.activation(warm[:, 1:2], warm[:, 0:1], SILU)
+        if "T" in MODES:
+            ident = keep.tile([P, P], F32, name="ident")
+            make_identity(nc, ident[:])
+
+        pending = []
+        for e in range(E):
+            lst = offsets[:, e * (C // 16) : (e + 1) * (C // 16)]
+            gs = keep.tile([P, C], U8, name=f"gs{e}", align_bytes=64)
+            gw = keep.tile([P, C], U32, name=f"gw{e}", align_bytes=64)
+            nc.vector.tensor_copy(gs[:], xs[:].indirect(lst))
+            nc.vector.tensor_copy(gw[:], xw[:].bitcast(U32).indirect(lst))
+            hb = keep.tile([P, C, 4], BF16, name=f"hb{e}", align_bytes=64)
+            if MODES[e] == "P":
+                pw = keep.tile([P, 2 * H], U8, name=f"pw{e}", align_bytes=64)
+                ps = keep.tile([P, H], U8, name=f"ps{e}", align_bytes=64)
+                nc.vector.tensor_copy(
+                    pw[:].bitcast(U16).rearrange("p (t m) -> p t m", t=4),
+                    w1w[:, e, :].bitcast(U16).rearrange("p (m t) -> p t m", t=4),
+                )
+                nc.vector.tensor_copy(
+                    ps[:].rearrange("p (t m) -> p t m", t=4),
+                    w1s[:, e, :].rearrange("p (m t) -> p t m", t=4),
+                )
+                for b in range(C // B):
+                    cols = slice(b * B, (b + 1) * B)
+                    a = psum.tile([P, 4, B], F32, name="a", tag="a", bufs=4)
+                    for t in range(4):
+                        nc.tensor.matmul_mx(
+                            out=a[:, t, :],
+                            lhsT=pw[:, 2 * P * t : 2 * P * (t + 1)].bitcast(FP4X4),
+                            lhsT_scale=ps[:, P * t : P * (t + 1)],
+                            rhs=gw[:, cols].bitcast(FP8X4),
+                            rhs_scale=gs[:, cols],
+                            start=True,
+                            stop=True,
+                        )
+                    nc.scalar.activation(hb[:, cols, :], a[:].rearrange("p t n -> p n t"), SILU)
+            else:
+                turned = psum.tile([P, 2, C], F32, name="turned", tag="turned", bufs=2)
+                for b in range(C // B):
+                    cols = slice(b * B, (b + 1) * B)
+                    a = psum.tile([P, 4, B], F32, name="a", tag="a", bufs=4)
+                    flat = a[:].rearrange("p t n -> p (t n)")
+                    nc.tensor.matmul_mx(
+                        out=flat,
+                        lhsT=gw[:, cols].bitcast(FP8X4),
+                        lhsT_scale=gs[:, cols],
+                        rhs=w1w[:, e, :].bitcast(FP4X4),
+                        rhs_scale=w1s[:, e, :],
+                        start=True,
+                        stop=True,
+                    )
+                    ht = keep.tile([P, H], BF16, name=f"ht{e}_{b}", align_bytes=64)
+                    nc.scalar.activation(
+                        ht[:].rearrange("s (u p v) -> s u p v", u=2, v=2),
+                        flat.rearrange("s (p u v) -> s u p v", u=2, v=2),
+                        SILU,
+                    )
+                    for u in range(2):
+                        nc.tensor.transpose(turned[:, u, cols], ht[:].bitcast(F32)[:, u * P : (u + 1) * P], ident[:])
+                nc.scalar.copy(
+                    hb[:].rearrange("p n t -> p (n t)").bitcast(F32).rearrange("p (n u) -> p n u", u=2),
+                    turned[:].rearrange("p u n -> p n u"),
+                )
+            hw = keep.tile([P, C], U32, name=f"hw{e}", align_bytes=64)
+            hs = keep.tile([P, C], U8, name=f"hs{e}", align_bytes=64)
+            nc.vector.quantize_mx(out=hw[:].bitcast(FP8X4), scales=hs[:], in_=hb[:].rearrange("p n t -> p (n t)"))
+            y = psum.tile([P, C], F32, name="y", tag="y", bufs=2)
+            nc.tensor.matmul_mx(
+                out=y[:],
+                lhsT=w2w[:, e, :].bitcast(FP4X4),
+                lhsT_scale=w2s[:, e, :],
+                rhs=hw[:].bitcast(FP8X4),
+                rhs_scale=hs[:],
+                start=True,
+                stop=True,
+            )
+            ysb = keep.tile([P, C], F32, name=f"ysb{e}")
+            gcols = gate_sb[:, e * C : (e + 1) * C]
+            if SCAT[e] == "d":
+                nc.scalar.copy(ysb[:], y[:])
+            else:
+                nc.vector.tensor_tensor(ysb[:], y[:], gcols, MULT)
+            pending.append((e, lst, ysb, gcols))
+
+        for e, lst, ysb, gcols in pending:
+            if SCAT[e] == "d":
+                nc.vector.tensor_tensor(window[:].indirect(lst), ysb[:], gcols, MULT)
+            else:
+                nc.vector.tensor_copy(window[:].indirect(lst), ysb[:])
+
+        c0 = 0
+        for i, width in enumerate(PIECES):
+            cols = slice(c0, c0 + width)
+            total = keep.tile([P, width], F32, name=f"total{i}")
+            nc.vector.tensor_tensor(total[:], window[:, cols], resid[:, cols], ADD)
+            queue = nc.sync if i % 2 == 0 else nc.scalar
+            queue.dma_start(out[:, cols], total[:])
+            c0 += width

@@ -21,7 +21,7 @@ ADD = mybir.AluOpType.add
 P = 128
 B = 128
 MODES = "TTTT"
-SCAT = "dddd"
+LAG = [1,2]
 PIECES = [512,512,256]
 
 
@@ -45,46 +45,49 @@ def tile_moe_res_mlp_silu_kernel(
         window = keep.tile([P, T], F32, name="window")
         warm = keep.tile([P, 8], F32, name="warm")
 
+        nc.vector.memset(warm[:], 0.0)
         nc.vector.memset(w1s[:].rearrange("p e c -> p (e c)").bitcast(I32), 0)
         nc.vector.memset(w2s[:].rearrange("p e c -> p (e c)").bitcast(I32), 0)
-        nc.vector.memset(warm[:], 0.0)
         nc.vector.memset(window[:], 0.0)
+
+        w1v = w1_words.rearrange("e o p c -> p (e o) c").bitcast(I32)
+
+        def load_xs(queue, q):
+            rows = x_scales[0, 4 * q : 4 * q + 4, :].bitcast(I32)
+            queue.dma_start(xs[32 * q : 32 * q + 32, :].bitcast(I32), rows.unsqueeze(0).to_broadcast([8, 4, T // 4]))
+
+        def load_plane(queue, plane, scales, q):
+            queue.dma_start(
+                plane[32 * q : 32 * q + 4, :, :].bitcast(I32),
+                scales[:, 0, 4 * q : 4 * q + 4, :].rearrange("e j c -> j e c").bitcast(I32),
+            )
 
         nc.sync.dma_start(offsets[:], offs)
         for q in range(4):
-            rows = x_scales[0, 4 * q : 4 * q + 4, :].bitcast(I32)
-            nc.sync.dma_start(xs[32 * q : 32 * q + 32, :].bitcast(I32), rows.unsqueeze(0).to_broadcast([8, 4, T // 4]))
+            load_xs(nc.scalar, q)
         nc.sync.dma_start(xw[:], x_words[0].rearrange("p t r -> p (t r)").bitcast(I32))
-        w1v = w1_words.rearrange("e o p c -> p (e o) c").bitcast(I32)
         nc.sync.dma_start(w1w[:, 0:1, :].bitcast(I32), w1v[:, 0:1, :])
         for q in range(4):
-            nc.sync.dma_start(
-                w1s[32 * q : 32 * q + 4, :, :].bitcast(I32),
-                w1_scales[:, 0, 4 * q : 4 * q + 4, :].rearrange("e j c -> j e c").bitcast(I32),
-            )
+            load_plane(nc.sync, w1s, w1_scales, q)
+        nc.scalar.activation(warm[:, 1:2], warm[:, 0:1], SILU)
         nc.sync.dma_start(w1w[:, 1:E, :].bitcast(I32), w1v[:, 1:E, :])
-        nc.sync.dma_start(w2w[:].bitcast(I32), w2_words.rearrange("e o p c -> p (e o) c").bitcast(I32))
+        nc.scalar.dma_start(w2w[:].bitcast(I32), w2_words.rearrange("e o p c -> p (e o) c").bitcast(I32))
         for q in range(4):
-            nc.sync.dma_start(
-                w2s[32 * q : 32 * q + 4, :, :].bitcast(I32),
-                w2_scales[:, 0, 4 * q : 4 * q + 4, :].rearrange("e j c -> j e c").bitcast(I32),
-            )
+            load_plane(nc.scalar, w2s, w2_scales, q)
         nc.sync.dma_start(gate_sb[:], gate)
         nc.sync.dma_start(resid[:], xr)
 
-        nc.scalar.activation(warm[:, 1:2], warm[:, 0:1], SILU)
         if "T" in MODES:
             ident = keep.tile([P, P], F32, name="ident")
             make_identity(nc, ident[:])
 
-        pending = []
-        for e in range(E):
+        def first_half(e):
             lst = offsets[:, e * (C // 16) : (e + 1) * (C // 16)]
             gs = keep.tile([P, C], U8, name=f"gs{e}", align_bytes=64)
             gw = keep.tile([P, C], U32, name=f"gw{e}", align_bytes=64)
             nc.vector.tensor_copy(gs[:], xs[:].indirect(lst))
             nc.vector.tensor_copy(gw[:], xw[:].bitcast(U32).indirect(lst))
-            hb = keep.tile([P, C, 4], BF16, name=f"hb{e}", align_bytes=64)
+            hb = keep.tile([P, C, 4], BF16, name=f"hb{e}", tag=f"slot{e}", align_bytes=64)
             if MODES[e] == "P":
                 pw = keep.tile([P, 2 * H], U8, name=f"pw{e}", align_bytes=64)
                 ps = keep.tile([P, H], U8, name=f"ps{e}", align_bytes=64)
@@ -150,19 +153,21 @@ def tile_moe_res_mlp_silu_kernel(
                 start=True,
                 stop=True,
             )
-            ysb = keep.tile([P, C], F32, name=f"ysb{e}")
-            gcols = gate_sb[:, e * C : (e + 1) * C]
-            if SCAT[e] == "d":
-                nc.scalar.copy(ysb[:], y[:])
-            else:
-                nc.vector.tensor_tensor(ysb[:], y[:], gcols, MULT)
-            pending.append((e, lst, ysb, gcols))
+            return y
 
-        for e, lst, ysb, gcols in pending:
-            if SCAT[e] == "d":
-                nc.vector.tensor_tensor(window[:].indirect(lst), ysb[:], gcols, MULT)
-            else:
-                nc.vector.tensor_copy(window[:].indirect(lst), ysb[:])
+        def second_half(e, y):
+            lst = offsets[:, e * (C // 16) : (e + 1) * (C // 16)]
+            ysb = keep.tile([P, C], F32, name=f"ysb{e}", tag=f"slot{e + 1 if e in LAG else e + E}", align_bytes=64)
+            gcols = gate_sb[:, e * C : (e + 1) * C]
+            nc.vector.tensor_tensor(ysb[:], y[:], gcols, MULT)
+            nc.vector.tensor_copy(window[:].indirect(lst), ysb[:])
+
+        sums = first_half(0)
+        for e in range(1, E):
+            ahead = first_half(e)
+            second_half(e - 1, sums)
+            sums = ahead
+        second_half(E - 1, sums)
 
         c0 = 0
         for i, width in enumerate(PIECES):

@@ -20,9 +20,9 @@ ADD = mybir.AluOpType.add
 
 P = 128
 B = 128
-MODES = "TTTT"
-LAG = [1,2]
-PIECES = [512,512,256]
+MODES = "TTTP"
+LAG = [0,1]
+PIECES = [384,384,256,256]
 
 
 def tile_moe_res_mlp_silu_kernel(
@@ -63,17 +63,22 @@ def tile_moe_res_mlp_silu_kernel(
             )
 
         nc.sync.dma_start(offsets[:], offs)
-        for q in range(4):
-            load_xs(nc.scalar, q)
+        load_xs(nc.scalar, 2)
+        load_xs(nc.sync, 0)
+        load_xs(nc.scalar, 3)
+        load_xs(nc.sync, 1)
         nc.sync.dma_start(xw[:], x_words[0].rearrange("p t r -> p (t r)").bitcast(I32))
+        for q in range(4):
+            load_plane(nc.scalar, w1s, w1_scales, q)
         nc.sync.dma_start(w1w[:, 0:1, :].bitcast(I32), w1v[:, 0:1, :])
-        for q in range(4):
-            load_plane(nc.sync, w1s, w1_scales, q)
         nc.scalar.activation(warm[:, 1:2], warm[:, 0:1], SILU)
-        nc.sync.dma_start(w1w[:, 1:E, :].bitcast(I32), w1v[:, 1:E, :])
-        nc.scalar.dma_start(w2w[:].bitcast(I32), w2_words.rearrange("e o p c -> p (e o) c").bitcast(I32))
-        for q in range(4):
-            load_plane(nc.scalar, w2s, w2_scales, q)
+        nc.sync.dma_start(w1w[:, 1:2, :].bitcast(I32), w1v[:, 1:2, :])
+        nc.sync.dma_start(w2w[:].bitcast(I32), w2_words.rearrange("e o p c -> p (e o) c").bitcast(I32))
+        load_plane(nc.scalar, w2s, w2_scales, 0)
+        load_plane(nc.sync, w2s, w2_scales, 1)
+        load_plane(nc.scalar, w2s, w2_scales, 2)
+        load_plane(nc.sync, w2s, w2_scales, 3)
+        nc.sync.dma_start(w1w[:, 2:E, :].bitcast(I32), w1v[:, 2:E, :])
         nc.sync.dma_start(gate_sb[:], gate)
         nc.sync.dma_start(resid[:], xr)
 
@@ -83,11 +88,11 @@ def tile_moe_res_mlp_silu_kernel(
 
         def first_half(e):
             lst = offsets[:, e * (C // 16) : (e + 1) * (C // 16)]
-            gs = keep.tile([P, C], U8, name=f"gs{e}", align_bytes=64)
+            gs = keep.tile([P, C], U8, name=f"gs{e}", tag="gs", bufs=2, align_bytes=64)
             gw = keep.tile([P, C], U32, name=f"gw{e}", align_bytes=64)
             nc.vector.tensor_copy(gs[:], xs[:].indirect(lst))
             nc.vector.tensor_copy(gw[:], xw[:].bitcast(U32).indirect(lst))
-            hb = keep.tile([P, C, 4], BF16, name=f"hb{e}", tag=f"slot{e}", align_bytes=64)
+            hb = keep.tile([P, C, 4], BF16, name=f"hb{e}", align_bytes=64)
             if MODES[e] == "P":
                 pw = keep.tile([P, 2 * H], U8, name=f"pw{e}", align_bytes=64)
                 ps = keep.tile([P, H], U8, name=f"ps{e}", align_bytes=64)
@@ -128,7 +133,7 @@ def tile_moe_res_mlp_silu_kernel(
                         start=True,
                         stop=True,
                     )
-                    ht = keep.tile([P, H], BF16, name=f"ht{e}_{b}", align_bytes=64)
+                    ht = keep.tile([P, H], BF16, name=f"ht{e}_{b}", tag=f"slot{e}" if b == 1 else f"ht{e}", align_bytes=64)
                     nc.scalar.activation(
                         ht[:].rearrange("s (u p v) -> s u p v", u=2, v=2),
                         flat.rearrange("s (p u v) -> s u p v", u=2, v=2),
@@ -157,11 +162,18 @@ def tile_moe_res_mlp_silu_kernel(
 
         def second_half(e, y):
             lst = offsets[:, e * (C // 16) : (e + 1) * (C // 16)]
-            ysb = keep.tile([P, C], F32, name=f"ysb{e}", tag=f"slot{e + 1 if e in LAG else e + E}", align_bytes=64)
-            gcols = gate_sb[:, e * C : (e + 1) * C]
-            nc.vector.tensor_tensor(ysb[:], y[:], gcols, MULT)
-            nc.vector.tensor_copy(window[:].indirect(lst), ysb[:])
+            if e < 2:
+                ysb = keep.tile([P, C], F32, name=f"ysb{e}", tag=f"slot{e + 1 if e in LAG else e + E}", align_bytes=64)
+                nc.scalar.copy(ysb[:], y[:])
+                nc.vector.tensor_tensor(window[:].indirect(lst), ysb[:], gate_sb[:, e * C : (e + 1) * C], MULT)
+            else:
+                nc.scalar.copy(ylast[:, (e - 2) * C : (e - 1) * C], y[:])
+                if e == E - 1:
+                    nc.vector.tensor_tensor(
+                        window[:].indirect(offsets[:, 2 * (C // 16) :]), ylast[:], gate_sb[:, 2 * C :], MULT
+                    )
 
+        ylast = keep.tile([P, 2 * C], F32, name="ylast")
         sums = first_half(0)
         for e in range(1, E):
             ahead = first_half(e)

@@ -1,7 +1,6 @@
 from contextlib import ExitStack
 
 import concourse.mybir as mybir
-from concourse.masks import make_identity
 
 K, T, E, C, H, N = 512, 1280, 4, 256, 512, 128
 FLOPS = 2 * E * C * (K * H + H * N)
@@ -19,10 +18,13 @@ MULT = mybir.AluOpType.mult
 ADD = mybir.AluOpType.add
 
 P = 128
-B = 128
-MODES = "TTTP"
-LAG = [0,1]
-PIECES = [384,384,256,256]
+PACK = 4
+QUADS = 4
+ROWS = 4
+W1_ROWS = QUADS * ROWS * E
+SLOTS = 128
+LIST_COLS = C // 16
+OUT_PIECES = (384, 384, 256, 256)
 
 
 def tile_moe_res_mlp_silu_kernel(
@@ -31,12 +33,14 @@ def tile_moe_res_mlp_silu_kernel(
     nc = tc.nc
     with ExitStack() as ctx:
         keep = ctx.enter_context(tc.tile_pool(name="keep", bufs=1))
-        psum = ctx.enter_context(tc.psum_pool(name="psum", bufs=1))
+        psum = ctx.enter_context(tc.psum_pool(name="psum", bufs=2))
 
-        offsets = keep.tile([P, E * C // 16], U16, name="offsets")
+        offsets = keep.tile([P, E * LIST_COLS], U16, name="offsets")
         xw = keep.tile([P, T], I32, name="xw", align_bytes=64)
         xs = keep.tile([P, T], U8, name="xs", align_bytes=64)
         w1w = keep.tile([P, E, 2 * H], U8, name="w1w", align_bytes=64)
+        w1s_rows = keep.tile([P, H], U8, name="w1s_rows", align_bytes=64)
+        w1s_regrouped = keep.tile([P, H], U8, name="w1s_regrouped", align_bytes=64)
         w1s = keep.tile([P, E, H], U8, name="w1s", align_bytes=64)
         w2w = keep.tile([P, E, 2 * N], U8, name="w2w", align_bytes=64)
         w2s = keep.tile([P, E, N], U8, name="w2s", align_bytes=64)
@@ -46,109 +50,88 @@ def tile_moe_res_mlp_silu_kernel(
         warm = keep.tile([P, 8], F32, name="warm")
 
         nc.vector.memset(warm[:], 0.0)
+        nc.vector.memset(w1s_rows[W1_ROWS:, :].bitcast(I32), 0)
         nc.vector.memset(w1s[:].rearrange("p e c -> p (e c)").bitcast(I32), 0)
         nc.vector.memset(w2s[:].rearrange("p e c -> p (e c)").bitcast(I32), 0)
         nc.vector.memset(window[:], 0.0)
 
-        w1v = w1_words.rearrange("e o p c -> p (e o) c").bitcast(I32)
-
-        def load_xs(queue, q):
-            rows = x_scales[0, 4 * q : 4 * q + 4, :].bitcast(I32)
-            queue.dma_start(xs[32 * q : 32 * q + 32, :].bitcast(I32), rows.unsqueeze(0).to_broadcast([8, 4, T // 4]))
-
-        def load_plane(queue, plane, scales, q):
+        def load_x_scales(queue, q):
+            rows = x_scales[0, ROWS * q : ROWS * (q + 1), :].bitcast(I32)
             queue.dma_start(
-                plane[32 * q : 32 * q + 4, :, :].bitcast(I32),
-                scales[:, 0, 4 * q : 4 * q + 4, :].rearrange("e j c -> j e c").bitcast(I32),
+                xs[32 * q : 32 * (q + 1), :].bitcast(I32),
+                rows.unsqueeze(0).to_broadcast([32 // ROWS, ROWS, T // 4]),
+            )
+
+        def load_w1_words(first, last):
+            words = w1_words.rearrange("e o p c -> p (e o) c").bitcast(I32)
+            nc.sync.dma_start(w1w[:, first:last, :].bitcast(I32), words[:, first:last, :])
+
+        def load_w2_scales(queue, q):
+            queue.dma_start(
+                w2s[32 * q : 32 * q + ROWS, :, :].bitcast(I32),
+                w2_scales[:, 0, ROWS * q : ROWS * (q + 1), :].rearrange("e j c -> j e c").bitcast(I32),
             )
 
         nc.sync.dma_start(offsets[:], offs)
-        load_xs(nc.scalar, 2)
-        load_xs(nc.sync, 0)
-        load_xs(nc.scalar, 3)
-        load_xs(nc.sync, 1)
+        for q in range(1, QUADS):
+            load_x_scales(nc.scalar, q)
+        nc.sync.dma_start(
+            w1s_rows[:W1_ROWS, :].bitcast(I32), w1_scales[:, 0, :, :].rearrange("e f c -> f e c").bitcast(I32)
+        )
+        nc.vector.tensor_copy(
+            w1s_regrouped[:].rearrange("r (t m) -> r t m", t=PACK),
+            w1s_rows[:].rearrange("r (m t) -> r t m", t=PACK),
+        )
+        load_x_scales(nc.sync, 0)
+        load_w1_words(0, 1)
         nc.sync.dma_start(xw[:], x_words[0].rearrange("p t r -> p (t r)").bitcast(I32))
-        for q in range(4):
-            load_plane(nc.scalar, w1s, w1_scales, q)
-        nc.sync.dma_start(w1w[:, 0:1, :].bitcast(I32), w1v[:, 0:1, :])
         nc.scalar.activation(warm[:, 1:2], warm[:, 0:1], SILU)
-        nc.sync.dma_start(w1w[:, 1:2, :].bitcast(I32), w1v[:, 1:2, :])
+        for q in range(QUADS):
+            nc.sync.dma_start(
+                w1s[32 * q : 32 * q + ROWS, :, :].bitcast(I32),
+                w1s_regrouped[ROWS * E * q : ROWS * E * (q + 1), :].bitcast(I32),
+            )
+        load_w1_words(1, 2)
+        load_w2_scales(nc.sync, 0)
+        for q in range(1, QUADS):
+            load_w2_scales(nc.scalar, q)
         nc.sync.dma_start(w2w[:].bitcast(I32), w2_words.rearrange("e o p c -> p (e o) c").bitcast(I32))
-        load_plane(nc.scalar, w2s, w2_scales, 0)
-        load_plane(nc.sync, w2s, w2_scales, 1)
-        load_plane(nc.scalar, w2s, w2_scales, 2)
-        load_plane(nc.sync, w2s, w2_scales, 3)
-        nc.sync.dma_start(w1w[:, 2:E, :].bitcast(I32), w1v[:, 2:E, :])
+        load_w1_words(2, E)
         nc.sync.dma_start(gate_sb[:], gate)
         nc.sync.dma_start(resid[:], xr)
 
-        if "T" in MODES:
-            ident = keep.tile([P, P], F32, name="ident")
-            make_identity(nc, ident[:])
+        def expert_list(e):
+            return offsets[:, e * LIST_COLS : (e + 1) * LIST_COLS]
 
-        def first_half(e):
-            lst = offsets[:, e * (C // 16) : (e + 1) * (C // 16)]
-            gs = keep.tile([P, C], U8, name=f"gs{e}", tag="gs", bufs=2, align_bytes=64)
+        def expert_sums(e):
+            gs = keep.tile([P, C], U8, name="gs", bufs=2, align_bytes=64)
             gw = keep.tile([P, C], U32, name=f"gw{e}", align_bytes=64)
-            nc.vector.tensor_copy(gs[:], xs[:].indirect(lst))
-            nc.vector.tensor_copy(gw[:], xw[:].bitcast(U32).indirect(lst))
-            hb = keep.tile([P, C, 4], BF16, name=f"hb{e}", align_bytes=64)
-            if MODES[e] == "P":
-                pw = keep.tile([P, 2 * H], U8, name=f"pw{e}", align_bytes=64)
-                ps = keep.tile([P, H], U8, name=f"ps{e}", align_bytes=64)
-                nc.vector.tensor_copy(
-                    pw[:].bitcast(U16).rearrange("p (t m) -> p t m", t=4),
-                    w1w[:, e, :].bitcast(U16).rearrange("p (m t) -> p t m", t=4),
-                )
-                nc.vector.tensor_copy(
-                    ps[:].rearrange("p (t m) -> p t m", t=4),
-                    w1s[:, e, :].rearrange("p (m t) -> p t m", t=4),
-                )
-                for b in range(C // B):
-                    cols = slice(b * B, (b + 1) * B)
-                    a = psum.tile([P, 4, B], F32, name="a", tag="a", bufs=4)
-                    for t in range(4):
-                        nc.tensor.matmul_mx(
-                            out=a[:, t, :],
-                            lhsT=pw[:, 2 * P * t : 2 * P * (t + 1)].bitcast(FP4X4),
-                            lhsT_scale=ps[:, P * t : P * (t + 1)],
-                            rhs=gw[:, cols].bitcast(FP8X4),
-                            rhs_scale=gs[:, cols],
-                            start=True,
-                            stop=True,
-                        )
-                    nc.scalar.activation(hb[:, cols, :], a[:].rearrange("p t n -> p n t"), SILU)
-            else:
-                turned = psum.tile([P, 2, C], F32, name="turned", tag="turned", bufs=2)
-                for b in range(C // B):
-                    cols = slice(b * B, (b + 1) * B)
-                    a = psum.tile([P, 4, B], F32, name="a", tag="a", bufs=4)
-                    flat = a[:].rearrange("p t n -> p (t n)")
+            nc.vector.tensor_copy(gs[:], xs[:].indirect(expert_list(e)))
+            nc.vector.tensor_copy(gw[:], xw[:].bitcast(U32).indirect(expert_list(e)))
+            w1g = keep.tile([P, 2 * H], U8, name=f"w1g{e}", align_bytes=64)
+            nc.vector.tensor_copy(
+                w1g[:].bitcast(U16).rearrange("p (t m) -> p t m", t=PACK),
+                w1w[:, e, :].bitcast(U16).rearrange("p (m t) -> p t m", t=PACK),
+            )
+            hb = keep.tile([P, C, PACK], BF16, name=f"hb{e}", align_bytes=64)
+            for s0 in range(0, C, SLOTS):
+                cols = slice(s0, s0 + SLOTS)
+                a = psum.tile([P, PACK, SLOTS], F32, name="a")
+                for t in range(PACK):
                     nc.tensor.matmul_mx(
-                        out=flat,
-                        lhsT=gw[:, cols].bitcast(FP8X4),
-                        lhsT_scale=gs[:, cols],
-                        rhs=w1w[:, e, :].bitcast(FP4X4),
-                        rhs_scale=w1s[:, e, :],
+                        out=a[:, t, :],
+                        lhsT=w1g[:, 2 * P * t : 2 * P * (t + 1)].bitcast(FP4X4),
+                        lhsT_scale=w1s[:, e, P * t : P * (t + 1)],
+                        rhs=gw[:, cols].bitcast(FP8X4),
+                        rhs_scale=gs[:, cols],
                         start=True,
                         stop=True,
                     )
-                    ht = keep.tile([P, H], BF16, name=f"ht{e}_{b}", tag=f"slot{e}" if b == 1 else f"ht{e}", align_bytes=64)
-                    nc.scalar.activation(
-                        ht[:].rearrange("s (u p v) -> s u p v", u=2, v=2),
-                        flat.rearrange("s (p u v) -> s u p v", u=2, v=2),
-                        SILU,
-                    )
-                    for u in range(2):
-                        nc.tensor.transpose(turned[:, u, cols], ht[:].bitcast(F32)[:, u * P : (u + 1) * P], ident[:])
-                nc.scalar.copy(
-                    hb[:].rearrange("p n t -> p (n t)").bitcast(F32).rearrange("p (n u) -> p n u", u=2),
-                    turned[:].rearrange("p u n -> p n u"),
-                )
+                nc.scalar.activation(hb[:, cols, :], a[:].rearrange("p t s -> p s t"), SILU)
             hw = keep.tile([P, C], U32, name=f"hw{e}", align_bytes=64)
             hs = keep.tile([P, C], U8, name=f"hs{e}", align_bytes=64)
-            nc.vector.quantize_mx(out=hw[:].bitcast(FP8X4), scales=hs[:], in_=hb[:].rearrange("p n t -> p (n t)"))
-            y = psum.tile([P, C], F32, name="y", tag="y", bufs=2)
+            nc.vector.quantize_mx(out=hw[:].bitcast(FP8X4), scales=hs[:], in_=hb[:].rearrange("p s t -> p (s t)"))
+            y = psum.tile([P, C], F32, name="y")
             nc.tensor.matmul_mx(
                 out=y[:],
                 lhsT=w2w[:, e, :].bitcast(FP4X4),
@@ -160,32 +143,25 @@ def tile_moe_res_mlp_silu_kernel(
             )
             return y
 
-        def second_half(e, y):
-            lst = offsets[:, e * (C // 16) : (e + 1) * (C // 16)]
-            if e < 2:
-                ysb = keep.tile([P, C], F32, name=f"ysb{e}", tag=f"slot{e + 1 if e in LAG else e + E}", align_bytes=64)
-                nc.scalar.copy(ysb[:], y[:])
-                nc.vector.tensor_tensor(window[:].indirect(lst), ysb[:], gate_sb[:, e * C : (e + 1) * C], MULT)
-            else:
-                nc.scalar.copy(ylast[:, (e - 2) * C : (e - 1) * C], y[:])
-                if e == E - 1:
-                    nc.vector.tensor_tensor(
-                        window[:].indirect(offsets[:, 2 * (C // 16) :]), ylast[:], gate_sb[:, 2 * C :], MULT
-                    )
+        def put_back(e, y):
+            y_sb = keep.tile([P, C], F32, name=f"y_sb{e}")
+            nc.scalar.copy(y_sb[:], y[:])
+            nc.vector.tensor_tensor(
+                window[:].indirect(expert_list(e)), y_sb[:], gate_sb[:, e * C : (e + 1) * C], MULT
+            )
 
-        ylast = keep.tile([P, 2 * C], F32, name="ylast")
-        sums = first_half(0)
+        sums = expert_sums(0)
         for e in range(1, E):
-            ahead = first_half(e)
-            second_half(e - 1, sums)
-            sums = ahead
-        second_half(E - 1, sums)
+            next_sums = expert_sums(e)
+            put_back(e - 1, sums)
+            sums = next_sums
+        put_back(E - 1, sums)
 
         c0 = 0
-        for i, width in enumerate(PIECES):
+        for piece, width in enumerate(OUT_PIECES):
             cols = slice(c0, c0 + width)
-            total = keep.tile([P, width], F32, name=f"total{i}")
+            total = keep.tile([P, width], F32, name=f"total{piece}")
             nc.vector.tensor_tensor(total[:], window[:, cols], resid[:, cols], ADD)
-            queue = nc.sync if i % 2 == 0 else nc.scalar
+            queue = nc.sync if piece % 2 == 0 else nc.scalar
             queue.dma_start(out[:, cols], total[:])
             c0 += width

@@ -24,6 +24,8 @@ ROWS = 4
 W1_ROWS = QUADS * ROWS * E
 SLOTS = 128
 LIST_COLS = C // 16
+W1_LOADS = ((0, 1), (1, 2), (2, 4))
+Y_BANK = (4, 5, 4, 5)
 OUT_PIECES = (384, 384, 256, 256)
 
 
@@ -33,27 +35,27 @@ def tile_moe_res_mlp_silu_kernel(
     nc = tc.nc
     with ExitStack() as ctx:
         keep = ctx.enter_context(tc.tile_pool(name="keep", bufs=1))
-        psum = ctx.enter_context(tc.psum_pool(name="psum", bufs=2))
+        psum = ctx.enter_context(tc.psum_pool(name="psum", bufs=1))
 
+        reused = ctx.enter_context(tc.tile_pool(name="reused", bufs=1))
+        banks = [psum.tile([P, PACK * SLOTS], F32, name=f"bank{b}") for b in range(6)]
         offsets = keep.tile([P, E * LIST_COLS], U16, name="offsets")
         xw = keep.tile([P, T], I32, name="xw", align_bytes=64)
         xs = keep.tile([P, T], U8, name="xs", align_bytes=64)
-        w1w = keep.tile([P, E, 2 * H], U8, name="w1w", align_bytes=64)
+        w1w = [keep.tile([P, last - first, 2 * H], U8, name=f"w1w{first}", align_bytes=64) for first, last in W1_LOADS]
         w1s_rows = keep.tile([P, H], U8, name="w1s_rows", align_bytes=64)
         w1s_regrouped = keep.tile([P, H], U8, name="w1s_regrouped", align_bytes=64)
         w1s = keep.tile([P, E, H], U8, name="w1s", align_bytes=64)
         w2w = keep.tile([P, E, 2 * N], U8, name="w2w", align_bytes=64)
-        w2s = keep.tile([P, E, N], U8, name="w2s", align_bytes=64)
-        gate_sb = keep.tile([P, E * C], F32, name="gate_sb")
+        w2s = w1s_rows[:].rearrange("p (e c) -> p e c", e=E)
+        gate_sb = [keep.tile([P, 2 * C], F32, name=f"gate_sb{h}") for h in range(E // 2)]
         resid = keep.tile([P, T], F32, name="resid")
         window = keep.tile([P, T], F32, name="window")
         warm = keep.tile([P, 8], F32, name="warm")
 
-        nc.vector.memset(warm[:], 0.0)
         nc.vector.memset(w1s_rows[W1_ROWS:, :].bitcast(I32), 0)
         nc.vector.memset(w1s[:].rearrange("p e c -> p (e c)").bitcast(I32), 0)
-        nc.vector.memset(w2s[:].rearrange("p e c -> p (e c)").bitcast(I32), 0)
-        nc.vector.memset(window[:], 0.0)
+        nc.gpsimd.memset(window[:], 0.0)
 
         def load_x_scales(queue, q):
             rows = x_scales[0, ROWS * q : ROWS * (q + 1), :].bitcast(I32)
@@ -62,78 +64,96 @@ def tile_moe_res_mlp_silu_kernel(
                 rows.unsqueeze(0).to_broadcast([32 // ROWS, ROWS, T // 4]),
             )
 
-        def load_w1_words(first, last):
+        def load_w1_words(h):
             words = w1_words.rearrange("e o p c -> p (e o) c").bitcast(I32)
-            nc.sync.dma_start(w1w[:, first:last, :].bitcast(I32), words[:, first:last, :])
-
-        def load_w2_scales(queue, q):
-            queue.dma_start(
-                w2s[32 * q : 32 * q + ROWS, :, :].bitcast(I32),
-                w2_scales[:, 0, ROWS * q : ROWS * (q + 1), :].rearrange("e j c -> j e c").bitcast(I32),
-            )
+            nc.sync.dma_start(w1w[h][:].bitcast(I32), words[:, W1_LOADS[h][0] : W1_LOADS[h][1], :])
 
         nc.sync.dma_start(offsets[:], offs)
-        for q in range(1, QUADS):
-            load_x_scales(nc.scalar, q)
-        nc.sync.dma_start(
+        nc.scalar.dma_start(
             w1s_rows[:W1_ROWS, :].bitcast(I32), w1_scales[:, 0, :, :].rearrange("e f c -> f e c").bitcast(I32)
         )
         nc.vector.tensor_copy(
             w1s_regrouped[:].rearrange("r (t m) -> r t m", t=PACK),
             w1s_rows[:].rearrange("r (m t) -> r t m", t=PACK),
         )
-        load_x_scales(nc.sync, 0)
-        load_w1_words(0, 1)
-        nc.sync.dma_start(xw[:], x_words[0].rearrange("p t r -> p (t r)").bitcast(I32))
-        nc.scalar.activation(warm[:, 1:2], warm[:, 0:1], SILU)
         for q in range(QUADS):
-            nc.sync.dma_start(
+            load_x_scales(nc.sync if q < 2 else nc.scalar, q)
+        load_w1_words(0)
+        nc.sync.dma_start(xw[:], x_words[0].rearrange("p t r -> p (t r)").bitcast(I32))
+        load_w1_words(1)
+        nc.scalar.activation(warm[:, 0:1], window[:, 0:1], SILU)
+        for q in range(QUADS):
+            queue = nc.sync if q < 2 else nc.scalar
+            queue.dma_start(
                 w1s[32 * q : 32 * q + ROWS, :, :].bitcast(I32),
                 w1s_regrouped[ROWS * E * q : ROWS * E * (q + 1), :].bitcast(I32),
             )
-        load_w1_words(1, 2)
-        load_w2_scales(nc.sync, 0)
-        for q in range(1, QUADS):
-            load_w2_scales(nc.scalar, q)
-        nc.sync.dma_start(w2w[:].bitcast(I32), w2_words.rearrange("e o p c -> p (e o) c").bitcast(I32))
-        load_w1_words(2, E)
-        nc.sync.dma_start(gate_sb[:], gate)
+        load_w1_words(2)
+        w1g = []
+
+        def regroup_w1(e):
+            w1g.append(keep.tile([P, 2 * H], U8, name=f"w1g{e}", align_bytes=64))
+            regroup = nc.scalar.copy if e < 2 else nc.vector.tensor_copy
+            regroup(
+                w1g[e][:].bitcast(U16).rearrange("p (t m) -> p t m", t=PACK),
+                w1w[min(e, 2)][:, max(e - 2, 0), :].bitcast(U16).rearrange("p (m t) -> p t m", t=PACK),
+            )
+
+        regroup_w1(0)
+        for q in range(QUADS):
+            queue = nc.scalar if q < 2 else nc.sync
+            queue.dma_start(
+                w2s[32 * q : 32 * q + ROWS, :, :].bitcast(I32),
+                w2_scales[:, 0, ROWS * q : ROWS * (q + 1), :].rearrange("e j c -> j e c").bitcast(I32),
+            )
+        nc.scalar.dma_start(w2w[:].bitcast(I32), w2_words.rearrange("e o p c -> p (e o) c").bitcast(I32))
+        for e in range(1, E):
+            regroup_w1(e)
+        for h in range(E // 2):
+            nc.sync.dma_start(gate_sb[h][:], gate[:, 2 * C * h : 2 * C * (h + 1)])
         nc.sync.dma_start(resid[:], xr)
 
         def expert_list(e):
             return offsets[:, e * LIST_COLS : (e + 1) * LIST_COLS]
 
         def expert_sums(e):
-            gs = keep.tile([P, C], U8, name="gs", bufs=2, align_bytes=64)
+            last = e == E - 1
+            if last:
+                gs = reused.tile([P, C], U8, name=f"gs{e}", align_bytes=64, offset=0)
+            elif e % 2 == 0:
+                gs = reused.tile([P, C], U8, name=f"gs{e}", align_bytes=64, offset=2048)
+            else:
+                gs = keep.tile([P, C], U8, name=f"gs{e}", align_bytes=64)
             gw = keep.tile([P, C], U32, name=f"gw{e}", align_bytes=64)
             nc.vector.tensor_copy(gs[:], xs[:].indirect(expert_list(e)))
             nc.vector.tensor_copy(gw[:], xw[:].bitcast(U32).indirect(expert_list(e)))
-            w1g = keep.tile([P, 2 * H], U8, name=f"w1g{e}", align_bytes=64)
-            nc.vector.tensor_copy(
-                w1g[:].bitcast(U16).rearrange("p (t m) -> p t m", t=PACK),
-                w1w[:, e, :].bitcast(U16).rearrange("p (m t) -> p t m", t=PACK),
-            )
-            hb = keep.tile([P, C, PACK], BF16, name=f"hb{e}", align_bytes=64)
-            for s0 in range(0, C, SLOTS):
-                cols = slice(s0, s0 + SLOTS)
-                a = psum.tile([P, PACK, SLOTS], F32, name="a")
+            if e == 0:
+                hb = reused.tile([P, C, PACK], BF16, name=f"hb{e}", align_bytes=64, offset=0)
+            else:
+                hb = keep.tile([P, C, PACK], BF16, name=f"hb{e}", align_bytes=64)
+            for b in range(C // SLOTS):
+                cols = slice(b * SLOTS, (b + 1) * SLOTS)
+                a = banks[2 * min(e, 1) + b][:].rearrange("p (t s) -> p t s", t=PACK)
                 for t in range(PACK):
                     nc.tensor.matmul_mx(
                         out=a[:, t, :],
-                        lhsT=w1g[:, 2 * P * t : 2 * P * (t + 1)].bitcast(FP4X4),
+                        lhsT=w1g[e][:, 2 * P * t : 2 * P * (t + 1)].bitcast(FP4X4),
                         lhsT_scale=w1s[:, e, P * t : P * (t + 1)],
                         rhs=gw[:, cols].bitcast(FP8X4),
                         rhs_scale=gs[:, cols],
                         start=True,
                         stop=True,
                     )
-                nc.scalar.activation(hb[:, cols, :], a[:].rearrange("p t s -> p s t"), SILU)
+                nc.scalar.activation(hb[:, cols, :], a.rearrange("p t s -> p s t"), SILU)
             hw = keep.tile([P, C], U32, name=f"hw{e}", align_bytes=64)
             hs = keep.tile([P, C], U8, name=f"hs{e}", align_bytes=64)
             nc.vector.quantize_mx(out=hw[:].bitcast(FP8X4), scales=hs[:], in_=hb[:].rearrange("p s t -> p (s t)"))
-            y = psum.tile([P, C], F32, name="y")
+            return hw, hs
+
+        def second_layer(e, hw, hs):
+            y = banks[Y_BANK[e]][:, :C]
             nc.tensor.matmul_mx(
-                out=y[:],
+                out=y,
                 lhsT=w2w[:, e, :].bitcast(FP4X4),
                 lhsT_scale=w2s[:, e, :],
                 rhs=hw[:].bitcast(FP8X4),
@@ -141,21 +161,18 @@ def tile_moe_res_mlp_silu_kernel(
                 start=True,
                 stop=True,
             )
-            return y
-
-        def put_back(e, y):
             y_sb = keep.tile([P, C], F32, name=f"y_sb{e}")
-            nc.scalar.copy(y_sb[:], y[:])
+            nc.scalar.copy(y_sb[:], y)
             nc.vector.tensor_tensor(
-                window[:].indirect(expert_list(e)), y_sb[:], gate_sb[:, e * C : (e + 1) * C], MULT
+                window[:].indirect(expert_list(e)), y_sb[:], gate_sb[e // 2][:, (e % 2) * C : (e % 2 + 1) * C], MULT
             )
 
-        sums = expert_sums(0)
+        h = expert_sums(0)
         for e in range(1, E):
-            next_sums = expert_sums(e)
-            put_back(e - 1, sums)
-            sums = next_sums
-        put_back(E - 1, sums)
+            next_h = expert_sums(e)
+            second_layer(e - 1, *h)
+            h = next_h
+        second_layer(E - 1, *h)
 
         c0 = 0
         for piece, width in enumerate(OUT_PIECES):

@@ -24,8 +24,11 @@ ROWS = 4
 W1_ROWS = QUADS * ROWS * E
 SLOTS = 128
 LIST_COLS = C // 16
-W1_LOADS = ((0, 1), (1, 2), (2, 4))
-Y_BANK = (4, 5, 4, 5)
+BYTE_CUTS = (0, 2, 5, 8)
+WORD_CUTS = (0, 160, 512, 768)
+W1_LOADS = ((0, 1), (1, 2), (2, 3), (3, 4))
+A_BANK = (0, 1, 2, 3, 0, 1, 4, 1)
+Y_BANK = (5, 0, 4, 2)
 OUT_PIECES = (384, 384, 256, 256)
 
 
@@ -36,15 +39,20 @@ def tile_moe_res_mlp_silu_kernel(
     with ExitStack() as ctx:
         keep = ctx.enter_context(tc.tile_pool(name="keep", bufs=1))
         psum = ctx.enter_context(tc.psum_pool(name="psum", bufs=1))
-
         reused = ctx.enter_context(tc.tile_pool(name="reused", bufs=1))
         banks = [psum.tile([P, PACK * SLOTS], F32, name=f"bank{b}") for b in range(6)]
         offsets = keep.tile([P, E * LIST_COLS], U16, name="offsets")
         xw = keep.tile([P, T], I32, name="xw", align_bytes=64)
         xs = keep.tile([P, T], U8, name="xs", align_bytes=64)
-        w1w = [keep.tile([P, last - first, 2 * H], U8, name=f"w1w{first}", align_bytes=64) for first, last in W1_LOADS]
+        GS_AT, HB_AT, RAW1_AT, HW0_AT = 0, (512, 2560), 512, 4608
+        w1w = [
+            keep.tile([P, 1, 2 * H], U8, name="w1w0", align_bytes=64),
+            reused.tile([P, 1, 2 * H], U8, name="w1w1", align_bytes=64, offset=RAW1_AT),
+            keep.tile([P, 1, 2 * H], U8, name="w1w2", align_bytes=64),
+            keep.tile([P, 1, 2 * H], U8, name="w1w3", align_bytes=64),
+        ]
         w1s_rows = keep.tile([P, H], U8, name="w1s_rows", align_bytes=64)
-        w1s_regrouped = keep.tile([P, H], U8, name="w1s_regrouped", align_bytes=64)
+        w1s_regrouped = reused.tile([P, H], U8, name="w1s_regrouped", align_bytes=64, offset=0)
         w1s = keep.tile([P, E, H], U8, name="w1s", align_bytes=64)
         w2w = keep.tile([P, E, 2 * N], U8, name="w2w", align_bytes=64)
         w2s = w1s_rows[:].rearrange("p (e c) -> p e c", e=E)
@@ -68,6 +76,10 @@ def tile_moe_res_mlp_silu_kernel(
             words = w1_words.rearrange("e o p c -> p (e o) c").bitcast(I32)
             nc.sync.dma_start(w1w[h][:].bitcast(I32), words[:, W1_LOADS[h][0] : W1_LOADS[h][1], :])
 
+        def raw_w1(e):
+            h = max(i for i, (first, last) in enumerate(W1_LOADS) if first <= e)
+            return w1w[h][:, e - W1_LOADS[h][0], :]
+
         nc.sync.dma_start(offsets[:], offs)
         nc.scalar.dma_start(
             w1s_rows[:W1_ROWS, :].bitcast(I32), w1_scales[:, 0, :, :].rearrange("e f c -> f e c").bitcast(I32)
@@ -80,7 +92,6 @@ def tile_moe_res_mlp_silu_kernel(
             load_x_scales(nc.sync if q < 2 else nc.scalar, q)
         load_w1_words(0)
         nc.sync.dma_start(xw[:], x_words[0].rearrange("p t r -> p (t r)").bitcast(I32))
-        load_w1_words(1)
         nc.scalar.activation(warm[:, 0:1], window[:, 0:1], SILU)
         for q in range(QUADS):
             queue = nc.sync if q < 2 else nc.scalar
@@ -88,91 +99,127 @@ def tile_moe_res_mlp_silu_kernel(
                 w1s[32 * q : 32 * q + ROWS, :, :].bitcast(I32),
                 w1s_regrouped[ROWS * E * q : ROWS * E * (q + 1), :].bitcast(I32),
             )
+        load_w1_words(1)
         load_w1_words(2)
-        w1g = []
+        w1g = {}
 
-        def regroup_w1(e):
-            w1g.append(keep.tile([P, 2 * H], U8, name=f"w1g{e}", align_bytes=64))
-            regroup = nc.scalar.copy if e < 2 else nc.vector.tensor_copy
+        def regroup_w1(e, regroup, pool, **place):
+            w1g[e] = pool.tile([P, 2 * H], U8, name=f"w1g{e}", align_bytes=64, **place)
             regroup(
                 w1g[e][:].bitcast(U16).rearrange("p (t m) -> p t m", t=PACK),
-                w1w[min(e, 2)][:, max(e - 2, 0), :].bitcast(U16).rearrange("p (m t) -> p t m", t=PACK),
+                raw_w1(e).bitcast(U16).rearrange("p (m t) -> p t m", t=PACK),
             )
 
-        regroup_w1(0)
+        regroup_w1(0, nc.scalar.copy, keep)
+        nc.sync.dma_start(w2w[:].bitcast(I32), w2_words.rearrange("e o p c -> p (e o) c").bitcast(I32))
         for q in range(QUADS):
-            queue = nc.scalar if q < 2 else nc.sync
-            queue.dma_start(
+            nc.scalar.dma_start(
                 w2s[32 * q : 32 * q + ROWS, :, :].bitcast(I32),
                 w2_scales[:, 0, ROWS * q : ROWS * (q + 1), :].rearrange("e j c -> j e c").bitcast(I32),
             )
-        nc.scalar.dma_start(w2w[:].bitcast(I32), w2_words.rearrange("e o p c -> p (e o) c").bitcast(I32))
-        for e in range(1, E):
-            regroup_w1(e)
+        regroup_w1(1, nc.scalar.copy, keep)
+        load_w1_words(3)
         for h in range(E // 2):
             nc.sync.dma_start(gate_sb[h][:], gate[:, 2 * C * h : 2 * C * (h + 1)])
         nc.sync.dma_start(resid[:], xr)
 
-        def expert_list(e):
-            return offsets[:, e * LIST_COLS : (e + 1) * LIST_COLS]
+        def block_list(first, last):
+            return offsets[:, first * SLOTS // 16 : last * SLOTS // 16]
 
-        def expert_sums(e):
-            last = e == E - 1
-            if last:
-                gs = reused.tile([P, C], U8, name=f"gs{e}", align_bytes=64, offset=0)
-            elif e % 2 == 0:
-                gs = reused.tile([P, C], U8, name=f"gs{e}", align_bytes=64, offset=2048)
-            else:
-                gs = keep.tile([P, C], U8, name=f"gs{e}", align_bytes=64)
-            gw = keep.tile([P, C], U32, name=f"gw{e}", align_bytes=64)
-            nc.vector.tensor_copy(gs[:], xs[:].indirect(expert_list(e)))
-            nc.vector.tensor_copy(gw[:], xw[:].bitcast(U32).indirect(expert_list(e)))
+        gs, gw = {}, {}
+
+        def gather(dest, source, dtype, first, last, pool, **place):
+            tile = pool.tile([P, (last - first) * SLOTS], dtype, name=f"g{len(gs)}_{len(gw)}", align_bytes=64, **place)
+            nc.vector.tensor_copy(tile[:], source.indirect(block_list(first, last)))
+            for b in range(first, last):
+                dest[b] = tile[:, (b - first) * SLOTS : (b - first + 1) * SLOTS]
+
+        gather(gs, xs[:], U8, BYTE_CUTS[0], BYTE_CUTS[1], keep)
+        gather(gs, xs[:], U8, BYTE_CUTS[1], BYTE_CUTS[2], keep)
+        words = keep.tile([P, WORD_CUTS[-1]], U32, name="words", align_bytes=64)
+        for first, last in zip(WORD_CUTS, WORD_CUTS[1:]):
+            nc.vector.tensor_copy(words[:, first:last], xw[:].bitcast(U32).indirect(offsets[:, first // 16 : last // 16]))
+        for b in range(WORD_CUTS[-1] // SLOTS):
+            gw[b] = words[:, b * SLOTS : (b + 1) * SLOTS]
+        gather(gs, xs[:], U8, BYTE_CUTS[2], BYTE_CUTS[3], reused, offset=GS_AT)
+
+        def first_layer(e):
             if e == 0:
-                hb = reused.tile([P, C, PACK], BF16, name=f"hb{e}", align_bytes=64, offset=0)
+                hb = reused.tile([P, C, PACK], BF16, name=f"hb{e}", align_bytes=64, offset=HB_AT[e])
             else:
                 hb = keep.tile([P, C, PACK], BF16, name=f"hb{e}", align_bytes=64)
-            for b in range(C // SLOTS):
-                cols = slice(b * SLOTS, (b + 1) * SLOTS)
-                a = banks[2 * min(e, 1) + b][:].rearrange("p (t s) -> p t s", t=PACK)
+            for half in range(C // SLOTS):
+                b = e * C // SLOTS + half
+                a = banks[A_BANK[b]][:].rearrange("p (t s) -> p t s", t=PACK)
                 for t in range(PACK):
                     nc.tensor.matmul_mx(
                         out=a[:, t, :],
                         lhsT=w1g[e][:, 2 * P * t : 2 * P * (t + 1)].bitcast(FP4X4),
                         lhsT_scale=w1s[:, e, P * t : P * (t + 1)],
-                        rhs=gw[:, cols].bitcast(FP8X4),
-                        rhs_scale=gs[:, cols],
+                        rhs=gw[b].bitcast(FP8X4),
+                        rhs_scale=gs[b],
                         start=True,
                         stop=True,
                     )
-                nc.scalar.activation(hb[:, cols, :], a.rearrange("p t s -> p s t"), SILU)
-            hw = keep.tile([P, C], U32, name=f"hw{e}", align_bytes=64)
+                nc.scalar.activation(
+                    hb[:, half * SLOTS : (half + 1) * SLOTS, :], a.rearrange("p t s -> p s t"), SILU
+                )
+            if e > 0:
+                second_layer(e - 1)
+            return hb
+
+        codes, y_sb = {}, {}
+
+        def pieces(e):
+            width = SLOTS if e == 0 else C
+            return [slice(c, c + width) for c in range(0, C, width)]
+
+        def quantise(e, hb):
+            if e == 0:
+                hw = reused.tile([P, C], U32, name=f"hw{e}", align_bytes=64, offset=HW0_AT)
+            else:
+                hw = keep.tile([P, C], U32, name=f"hw{e}", align_bytes=64)
             hs = keep.tile([P, C], U8, name=f"hs{e}", align_bytes=64)
-            nc.vector.quantize_mx(out=hw[:].bitcast(FP8X4), scales=hs[:], in_=hb[:].rearrange("p s t -> p (s t)"))
-            return hw, hs
+            for cols in pieces(e):
+                nc.vector.quantize_mx(
+                    out=hw[:, cols].bitcast(FP8X4), scales=hs[:, cols], in_=hb[:, cols, :].rearrange("p s t -> p (s t)")
+                )
+            codes[e] = hw, hs
 
-        def second_layer(e, hw, hs):
+        def second_layer(e):
+            hw, hs = codes[e]
+            y_sb[e] = keep.tile([P, C], F32, name=f"y_sb{e}")
             y = banks[Y_BANK[e]][:, :C]
-            nc.tensor.matmul_mx(
-                out=y,
-                lhsT=w2w[:, e, :].bitcast(FP4X4),
-                lhsT_scale=w2s[:, e, :],
-                rhs=hw[:].bitcast(FP8X4),
-                rhs_scale=hs[:],
-                start=True,
-                stop=True,
-            )
-            y_sb = keep.tile([P, C], F32, name=f"y_sb{e}")
-            nc.scalar.copy(y_sb[:], y)
+            for cols in pieces(e):
+                nc.tensor.matmul_mx(
+                    out=y[:, cols],
+                    lhsT=w2w[:, e, :].bitcast(FP4X4),
+                    lhsT_scale=w2s[:, e, :],
+                    rhs=hw[:, cols].bitcast(FP8X4),
+                    rhs_scale=hs[:, cols],
+                    start=True,
+                    stop=True,
+                )
+            nc.scalar.copy(y_sb[e][:], y)
+
+        def scatter(e):
             nc.vector.tensor_tensor(
-                window[:].indirect(expert_list(e)), y_sb[:], gate_sb[e // 2][:, (e % 2) * C : (e % 2 + 1) * C], MULT
+                window[:].indirect(block_list(2 * e, 2 * e + 2)),
+                y_sb[e][:],
+                gate_sb[e // 2][:, (e % 2) * C : (e % 2 + 1) * C],
+                MULT,
             )
 
-        h = expert_sums(0)
+        quantise(0, first_layer(0))
+        regroup_w1(2, nc.vector.tensor_copy, reused, offset=HB_AT[0] + 2 * H)
+        gather(gw, xw[:].bitcast(U32), U32, 6, 8, reused, offset=HB_AT[0])
         for e in range(1, E):
-            next_h = expert_sums(e)
-            second_layer(e - 1, *h)
-            h = next_h
-        second_layer(E - 1, *h)
+            quantise(e, first_layer(e))
+            scatter(e - 1)
+            if e == 1:
+                regroup_w1(3, nc.scalar.copy, reused, offset=HW0_AT)
+        second_layer(E - 1)
+        scatter(E - 1)
 
         c0 = 0
         for piece, width in enumerate(OUT_PIECES):

@@ -29,7 +29,7 @@ WORD_CUTS = (0, 160, 512, 768)
 W1_LOADS = ((0, 1), (1, 2), (2, 3), (3, 4))
 A_BANK = (0, 1, 2, 3, 0, 1, 4, 1)
 Y_BANK = (5, 0, 4, 2)
-OUT_PIECES = (384, 384, 256, 256)
+OUT_PIECES = (160,) * 8
 
 
 def tile_moe_res_mlp_silu_kernel(

@@ -25,7 +25,7 @@ W1_ROWS = QUADS * ROWS * E
 SLOTS = 128
 LIST_COLS = C // 16
 BYTE_CUTS = (0, 2, 5, 8)
-WORD_CUTS = (0, 160, 512, 768)
+WORD_CUTS = (0, 160, 320, 512, 768)
 W1_LOADS = ((0, 1), (1, 2), (2, 3), (3, 4))
 A_BANK = (0, 1, 2, 3, 0, 1, 4, 1)
 Y_BANK = (5, 0, 4, 2)
@@ -56,7 +56,8 @@ def tile_moe_res_mlp_silu_kernel(
         w1s = keep.tile([P, E, H], U8, name="w1s", align_bytes=64)
         w2w = keep.tile([P, E, 2 * N], U8, name="w2w", align_bytes=64)
         w2s = w1s_rows[:].rearrange("p (e c) -> p e c", e=E)
-        gate_sb = [keep.tile([P, 2 * C], F32, name=f"gate_sb{h}") for h in range(E // 2)]
+        gate_first = keep.tile([P, C], F32, name="gate_first")
+        gate_rest = keep.tile([P, (E - 1) * C], F32, name="gate_rest")
         resid = keep.tile([P, T], F32, name="resid")
         window = keep.tile([P, T], F32, name="window")
         warm = keep.tile([P, 8], F32, name="warm")
@@ -119,8 +120,8 @@ def tile_moe_res_mlp_silu_kernel(
             )
         regroup_w1(1, nc.scalar.copy, keep)
         load_w1_words(3)
-        for h in range(E // 2):
-            nc.sync.dma_start(gate_sb[h][:], gate[:, 2 * C * h : 2 * C * (h + 1)])
+        nc.sync.dma_start(gate_first[:], gate[:, :C])
+        nc.sync.dma_start(gate_rest[:], gate[:, C:])
         nc.sync.dma_start(resid[:], xr)
 
         def block_list(first, last):
@@ -206,7 +207,7 @@ def tile_moe_res_mlp_silu_kernel(
             nc.vector.tensor_tensor(
                 window[:].indirect(block_list(2 * e, 2 * e + 2)),
                 y_sb[e][:],
-                gate_sb[e // 2][:, (e % 2) * C : (e % 2 + 1) * C],
+                gate_first[:] if e == 0 else gate_rest[:, (e - 1) * C : e * C],
                 MULT,
             )
 

@@ -24,7 +24,7 @@ ROWS = 4
 W1_ROWS = QUADS * ROWS * E
 SLOTS = 128
 LIST_COLS = C // 16
-BYTE_CUTS = (0, 2, 5, 8)
+BYTE_CUTS = (0, 2, 4, 8)
 WORD_CUTS = (0, 160, 320, 512, 768)
 W1_LOADS = ((0, 1), (1, 2), (2, 3), (3, 4))
 A_BANK = (0, 1, 2, 3, 0, 1, 4, 1)

@@ -14,6 +14,7 @@ U8 = mybir.dt.uint8
 FP8X4 = mybir.dt.float8_e4m3fn_x4
 FP4X4 = mybir.dt.float4_e2m1fn_x4
 SILU = mybir.ActivationFunctionType.Silu
+COPY = mybir.ActivationFunctionType.Copy
 MULT = mybir.AluOpType.mult
 ADD = mybir.AluOpType.add
 
@@ -23,12 +24,14 @@ QUADS = 4
 ROWS = 4
 W1_ROWS = QUADS * ROWS * E
 SLOTS = 128
-LIST_COLS = C // 16
-BYTE_CUTS = (0, 2, 4, 8)
-WORD_CUTS = (0, 160, 320, 512, 768)
-W1_LOADS = ((0, 1), (1, 2), (2, 3), (3, 4))
-A_BANK = (0, 1, 2, 3, 0, 1, 4, 1)
-Y_BANK = (5, 0, 4, 2)
+BYTE_CUTS = (0, 256, 640, 1024)
+WORD_CUTS = (0, 160, 320, 512, 768, 1024)
+W1_LOADS = ((0, 1), (1, 2), (2, 4))
+A_BANK = (0, 1, 2, 3, 4, 5, 3, 4)
+Y_BANK = (0, 1, 4, 2)
+VECTOR_PIECES = ((0, 160), (832, 1024))
+SCALAR_PIECES = ((160, 512), (512, 832))
+HW_AT = {}
 OUT_PIECES = (160,) * 8
 
 
@@ -41,30 +44,28 @@ def tile_moe_res_mlp_silu_kernel(
         psum = ctx.enter_context(tc.psum_pool(name="psum", bufs=1))
         reused = ctx.enter_context(tc.tile_pool(name="reused", bufs=1))
         banks = [psum.tile([P, PACK * SLOTS], F32, name=f"bank{b}") for b in range(6)]
-        offsets = keep.tile([P, E * LIST_COLS], U16, name="offsets")
-        xw = keep.tile([P, T], I32, name="xw", align_bytes=64)
+        offsets = keep.tile([P, E * C // 16], U16, name="offsets")
+        xw = reused.tile([P, T], I32, name="xw", align_bytes=64, offset=8192)
         xs = keep.tile([P, T], U8, name="xs", align_bytes=64)
-        GS_AT, HB_AT, RAW1_AT, HW0_AT = 0, (512, 2560), 512, 4608
         w1w = [
-            keep.tile([P, 1, 2 * H], U8, name="w1w0", align_bytes=64),
-            reused.tile([P, 1, 2 * H], U8, name="w1w1", align_bytes=64, offset=RAW1_AT),
-            keep.tile([P, 1, 2 * H], U8, name="w1w2", align_bytes=64),
-            keep.tile([P, 1, 2 * H], U8, name="w1w3", align_bytes=64),
+            reused.tile([P, 1, 2 * H], U8, name="w1w0", align_bytes=64, offset=0),
+            reused.tile([P, 1, 2 * H], U8, name="w1w1", align_bytes=64, offset=16384),
+            reused.tile([P, 2, 2 * H], U8, name="w1w2", align_bytes=64, offset=20480),
         ]
         w1s_rows = keep.tile([P, H], U8, name="w1s_rows", align_bytes=64)
-        w1s_regrouped = reused.tile([P, H], U8, name="w1s_regrouped", align_bytes=64, offset=0)
+        w1s_regrouped = reused.tile([P, H], U8, name="w1s_regrouped", align_bytes=64, offset=4 * T)
         w1s = keep.tile([P, E, H], U8, name="w1s", align_bytes=64)
         w2w = keep.tile([P, E, 2 * N], U8, name="w2w", align_bytes=64)
         w2s = w1s_rows[:].rearrange("p (e c) -> p e c", e=E)
-        gate_first = keep.tile([P, C], F32, name="gate_first")
-        gate_rest = keep.tile([P, (E - 1) * C], F32, name="gate_rest")
-        resid = keep.tile([P, T], F32, name="resid")
-        window = keep.tile([P, T], F32, name="window")
+        gate_first = keep.tile([P, 2 * C], F32, name="gate_first")
+        window_s = keep.tile([P, T], F32, name="window_s")
+        partial = keep.tile([P, T], F32, name="partial")
+        gated = keep.tile([P, E * C], F32, name="gated")
         warm = keep.tile([P, 8], F32, name="warm")
 
         nc.vector.memset(w1s_rows[W1_ROWS:, :].bitcast(I32), 0)
         nc.vector.memset(w1s[:].rearrange("p e c -> p (e c)").bitcast(I32), 0)
-        nc.gpsimd.memset(window[:], 0.0)
+        nc.gpsimd.memset(window_s[:], 0.0)
 
         def load_x_scales(queue, q):
             rows = x_scales[0, ROWS * q : ROWS * (q + 1), :].bitcast(I32)
@@ -73,9 +74,9 @@ def tile_moe_res_mlp_silu_kernel(
                 rows.unsqueeze(0).to_broadcast([32 // ROWS, ROWS, T // 4]),
             )
 
-        def load_w1_words(h):
+        def load_w1_words(h, queue):
             words = w1_words.rearrange("e o p c -> p (e o) c").bitcast(I32)
-            nc.sync.dma_start(w1w[h][:].bitcast(I32), words[:, W1_LOADS[h][0] : W1_LOADS[h][1], :])
+            queue.dma_start(w1w[h][:].bitcast(I32), words[:, W1_LOADS[h][0] : W1_LOADS[h][1], :])
 
         def raw_w1(e):
             h = max(i for i, (first, last) in enumerate(W1_LOADS) if first <= e)
@@ -91,142 +92,165 @@ def tile_moe_res_mlp_silu_kernel(
         )
         for q in range(QUADS):
             load_x_scales(nc.sync if q < 2 else nc.scalar, q)
-        load_w1_words(0)
+        load_w1_words(0, nc.sync)
         nc.sync.dma_start(xw[:], x_words[0].rearrange("p t r -> p (t r)").bitcast(I32))
-        nc.scalar.activation(warm[:, 0:1], window[:, 0:1], SILU)
+        nc.scalar.activation(warm[:, 0:1], window_s[:, 0:1], SILU)
         for q in range(QUADS):
             queue = nc.sync if q < 2 else nc.scalar
             queue.dma_start(
                 w1s[32 * q : 32 * q + ROWS, :, :].bitcast(I32),
                 w1s_regrouped[ROWS * E * q : ROWS * E * (q + 1), :].bitcast(I32),
             )
-        load_w1_words(1)
-        load_w1_words(2)
+        load_w1_words(1, nc.sync)
+        load_w1_words(2, nc.sync)
         w1g = {}
 
-        def regroup_w1(e, regroup, pool, **place):
-            w1g[e] = pool.tile([P, 2 * H], U8, name=f"w1g{e}", align_bytes=64, **place)
+        def regroup_w1(e, regroup):
+            w1g[e] = keep.tile([P, 2 * H], U8, name=f"w1g{e}", align_bytes=64)
             regroup(
                 w1g[e][:].bitcast(U16).rearrange("p (t m) -> p t m", t=PACK),
                 raw_w1(e).bitcast(U16).rearrange("p (m t) -> p t m", t=PACK),
             )
 
-        regroup_w1(0, nc.scalar.copy, keep)
+        regroup_w1(0, nc.scalar.copy)
+        window_v = reused.tile([P, T], F32, name="window_v", align_bytes=64, offset=0)
+        nc.gpsimd.memset(window_v[:], 0.0)
         nc.sync.dma_start(w2w[:].bitcast(I32), w2_words.rearrange("e o p c -> p (e o) c").bitcast(I32))
         for q in range(QUADS):
-            nc.scalar.dma_start(
+            queue = nc.sync if q < 2 else nc.scalar
+            queue.dma_start(
                 w2s[32 * q : 32 * q + ROWS, :, :].bitcast(I32),
                 w2_scales[:, 0, ROWS * q : ROWS * (q + 1), :].rearrange("e j c -> j e c").bitcast(I32),
             )
-        regroup_w1(1, nc.scalar.copy, keep)
-        load_w1_words(3)
-        nc.sync.dma_start(gate_first[:], gate[:, :C])
-        nc.sync.dma_start(gate_rest[:], gate[:, C:])
+        regroup_w1(1, nc.scalar.copy)
+        nc.sync.dma_start(gate_first[:], gate[:, : 2 * C])
+        gate_rest = reused.tile([P, 2 * C], F32, name="gate_rest", align_bytes=64, offset=16448)
+        nc.sync.dma_start(gate_rest[:], gate[:, 2 * C :])
+
+        def entries(first, last):
+            return offsets[:, first // 16 : last // 16]
+
+        gs_first = keep.tile([P, BYTE_CUTS[2]], U8, name="gs_first", align_bytes=64)
+        gs_last = reused.tile([P, E * C - BYTE_CUTS[2]], U8, name="gs_last", align_bytes=64, offset=4 * T)
+
+        def gs(first, last):
+            cut = BYTE_CUTS[2]
+            return gs_first[:, first:last] if first < cut else gs_last[:, first - cut : last - cut]
+
+        gw = keep.tile([P, E * C], U32, name="gw", align_bytes=64)
+
+        def gather_bytes(i):
+            first, last = BYTE_CUTS[i], BYTE_CUTS[i + 1]
+            nc.vector.tensor_copy(gs(first, last), xs[:].indirect(entries(first, last)))
+
+        def gather_words(i):
+            first, last = WORD_CUTS[i], WORD_CUTS[i + 1]
+            nc.vector.tensor_copy(gw[:, first:last], xw[:].bitcast(U32).indirect(entries(first, last)))
+
+        gather_bytes(0)
+        gather_bytes(1)
+        gather_words(0)
+        gather_words(1)
+        gather_words(2)
+        gather_bytes(2)
+        gather_words(3)
+        gather_words(4)
+        resid = reused.tile([P, T], F32, name="resid", align_bytes=64, offset=8192)
         nc.sync.dma_start(resid[:], xr)
+        w1g[2] = keep.tile([P, 2 * H], U8, name="w1g2", align_bytes=64)
+        nc.gpsimd.tensor_copy(
+            w1g[2][:].rearrange("p (t m b) -> p t m b", t=PACK, b=2),
+            raw_w1(2).rearrange("p (m t b) -> p t m b", t=PACK, b=2),
+        )
+        regroup_w1(3, nc.vector.tensor_copy)
 
-        def block_list(first, last):
-            return offsets[:, first * SLOTS // 16 : last * SLOTS // 16]
-
-        gs, gw = {}, {}
-
-        def gather(dest, source, dtype, first, last, pool, **place):
-            tile = pool.tile([P, (last - first) * SLOTS], dtype, name=f"g{len(gs)}_{len(gw)}", align_bytes=64, **place)
-            nc.vector.tensor_copy(tile[:], source.indirect(block_list(first, last)))
-            for b in range(first, last):
-                dest[b] = tile[:, (b - first) * SLOTS : (b - first + 1) * SLOTS]
-
-        gather(gs, xs[:], U8, BYTE_CUTS[0], BYTE_CUTS[1], keep)
-        gather(gs, xs[:], U8, BYTE_CUTS[1], BYTE_CUTS[2], keep)
-        words = keep.tile([P, WORD_CUTS[-1]], U32, name="words", align_bytes=64)
-        for first, last in zip(WORD_CUTS, WORD_CUTS[1:]):
-            nc.vector.tensor_copy(words[:, first:last], xw[:].bitcast(U32).indirect(offsets[:, first // 16 : last // 16]))
-        for b in range(WORD_CUTS[-1] // SLOTS):
-            gw[b] = words[:, b * SLOTS : (b + 1) * SLOTS]
-        gather(gs, xs[:], U8, BYTE_CUTS[2], BYTE_CUTS[3], reused, offset=GS_AT)
+        hb = {}
 
         def first_layer(e):
             if e == 0:
-                hb = reused.tile([P, C, PACK], BF16, name=f"hb{e}", align_bytes=64, offset=HB_AT[e])
+                hb[e] = reused.tile([P, C, PACK], BF16, name=f"hb{e}", align_bytes=64, offset=14400)
             else:
-                hb = keep.tile([P, C, PACK], BF16, name=f"hb{e}", align_bytes=64)
+                hb[e] = keep.tile([P, C, PACK], BF16, name=f"hb{e}", align_bytes=64)
             for half in range(C // SLOTS):
                 b = e * C // SLOTS + half
+                cols = slice(b * SLOTS, (b + 1) * SLOTS)
                 a = banks[A_BANK[b]][:].rearrange("p (t s) -> p t s", t=PACK)
                 for t in range(PACK):
                     nc.tensor.matmul_mx(
                         out=a[:, t, :],
                         lhsT=w1g[e][:, 2 * P * t : 2 * P * (t + 1)].bitcast(FP4X4),
                         lhsT_scale=w1s[:, e, P * t : P * (t + 1)],
-                        rhs=gw[b].bitcast(FP8X4),
-                        rhs_scale=gs[b],
+                        rhs=gw[:, cols].bitcast(FP8X4),
+                        rhs_scale=gs(b * SLOTS, (b + 1) * SLOTS),
                         start=True,
                         stop=True,
                     )
                 nc.scalar.activation(
-                    hb[:, half * SLOTS : (half + 1) * SLOTS, :], a.rearrange("p t s -> p s t"), SILU
+                    hb[e][:, half * SLOTS : (half + 1) * SLOTS, :], a.rearrange("p t s -> p s t"), SILU
                 )
-            if e > 0:
-                second_layer(e - 1)
-            return hb
 
-        codes, y_sb = {}, {}
+        codes = {}
 
-        def pieces(e):
-            width = SLOTS if e == 0 else C
-            return [slice(c, c + width) for c in range(0, C, width)]
-
-        def quantise(e, hb):
-            if e == 0:
-                hw = reused.tile([P, C], U32, name=f"hw{e}", align_bytes=64, offset=HW0_AT)
+        def quantise(e):
+            if e in HW_AT:
+                hw = reused.tile([P, C], U32, name=f"hw{e}", align_bytes=64, offset=HW_AT[e])
             else:
                 hw = keep.tile([P, C], U32, name=f"hw{e}", align_bytes=64)
             hs = keep.tile([P, C], U8, name=f"hs{e}", align_bytes=64)
-            for cols in pieces(e):
-                nc.vector.quantize_mx(
-                    out=hw[:, cols].bitcast(FP8X4), scales=hs[:, cols], in_=hb[:, cols, :].rearrange("p s t -> p (s t)")
-                )
+            nc.vector.quantize_mx(
+                out=hw[:].bitcast(FP8X4), scales=hs[:], in_=hb[e][:].rearrange("p s t -> p (s t)")
+            )
             codes[e] = hw, hs
 
         def second_layer(e):
             hw, hs = codes[e]
-            y_sb[e] = keep.tile([P, C], F32, name=f"y_sb{e}")
             y = banks[Y_BANK[e]][:, :C]
-            for cols in pieces(e):
-                nc.tensor.matmul_mx(
-                    out=y[:, cols],
-                    lhsT=w2w[:, e, :].bitcast(FP4X4),
-                    lhsT_scale=w2s[:, e, :],
-                    rhs=hw[:, cols].bitcast(FP8X4),
-                    rhs_scale=hs[:, cols],
-                    start=True,
-                    stop=True,
-                )
-            nc.scalar.copy(y_sb[e][:], y)
-
-        def scatter(e):
-            nc.vector.tensor_tensor(
-                window[:].indirect(block_list(2 * e, 2 * e + 2)),
-                y_sb[e][:],
-                gate_first[:] if e == 0 else gate_rest[:, (e - 1) * C : e * C],
-                MULT,
+            nc.tensor.matmul_mx(
+                out=y,
+                lhsT=w2w[:, e, :].bitcast(FP4X4),
+                lhsT_scale=w2s[:, e, :],
+                rhs=hw[:].bitcast(FP8X4),
+                rhs_scale=hs[:],
+                start=True,
+                stop=True,
             )
 
-        quantise(0, first_layer(0))
-        regroup_w1(2, nc.vector.tensor_copy, reused, offset=HB_AT[0] + 2 * H)
-        gather(gw, xw[:].bitcast(U32), U32, 6, 8, reused, offset=HB_AT[0])
-        for e in range(1, E):
-            quantise(e, first_layer(e))
-            scatter(e - 1)
-            if e == 1:
-                regroup_w1(3, nc.scalar.copy, reused, offset=HW0_AT)
-        second_layer(E - 1)
-        scatter(E - 1)
+        def gate_product(e):
+            cols = slice(e * C, (e + 1) * C)
+            nc.vector.tensor_tensor(gated[:, cols], banks[Y_BANK[e]][:, :C], (gate_first if e < 2 else gate_rest)[:, e % 2 * C : (e % 2 + 1) * C], MULT)
+
+        def scatter_on_vector(i):
+            first, last = VECTOR_PIECES[i]
+            nc.vector.tensor_copy(window_v[:].indirect(entries(first, last)), gated[:, first:last])
+
+        for e in range(E - 1):
+            first_layer(e)
+        quantise(0)
+        second_layer(0)
+        gate_product(0)
+        quantise(1)
+        second_layer(1)
+        first_layer(E - 1)
+        scatter_on_vector(0)
+        gate_product(1)
+        quantise(2)
+        quantise(3)
+        second_layer(2)
+        gate_product(2)
+        second_layer(3)
+        gate_product(3)
+        scatter_on_vector(1)
+        for first, last in SCALAR_PIECES:
+            nc.scalar.activation(window_s[:].indirect(entries(first, last)), gated[:, first:last], COPY)
+        for half in range(2):
+            cols = slice(half * T // 2, (half + 1) * T // 2)
+            nc.vector.tensor_tensor(partial[:, cols], window_v[:, cols], resid[:, cols], ADD)
 
         c0 = 0
         for piece, width in enumerate(OUT_PIECES):
             cols = slice(c0, c0 + width)
             total = keep.tile([P, width], F32, name=f"total{piece}")
-            nc.vector.tensor_tensor(total[:], window[:, cols], resid[:, cols], ADD)
+            nc.vector.tensor_tensor(total[:], window_s[:, cols], partial[:, cols], ADD)
             queue = nc.sync if piece % 2 == 0 else nc.scalar
             queue.dma_start(out[:, cols], total[:])
             c0 += width

@@ -157,11 +157,7 @@ def tile_moe_res_mlp_silu_kernel(
         gather_words(4)
         resid = reused.tile([P, T], F32, name="resid", align_bytes=64, offset=8192)
         nc.sync.dma_start(resid[:], xr)
-        w1g[2] = keep.tile([P, 2 * H], U8, name="w1g2", align_bytes=64)
-        nc.gpsimd.tensor_copy(
-            w1g[2][:].rearrange("p (t m b) -> p t m b", t=PACK, b=2),
-            raw_w1(2).rearrange("p (m t b) -> p t m b", t=PACK, b=2),
-        )
+        regroup_w1(2, nc.vector.tensor_copy)
         regroup_w1(3, nc.vector.tensor_copy)
 
         hb = {}

@@ -32,6 +32,7 @@ Y_BANK = (0, 1, 4, 2)
 VECTOR_PIECES = ((0, 160), (832, 1024))
 SCALAR_PIECES = ((160, 512), (512, 832))
 HW_AT = {}
+SEED = 256
 OUT_PIECES = (160,) * 8
 
 
@@ -59,13 +60,15 @@ def tile_moe_res_mlp_silu_kernel(
         w2s = w1s_rows[:].rearrange("p (e c) -> p e c", e=E)
         gate_first = keep.tile([P, 2 * C], F32, name="gate_first")
         window_s = keep.tile([P, T], F32, name="window_s")
+        window_v = keep.tile([P, T], F32, name="window_v")
         partial = keep.tile([P, T], F32, name="partial")
         gated = keep.tile([P, E * C], F32, name="gated")
         warm = keep.tile([P, 8], F32, name="warm")
 
         nc.vector.memset(w1s_rows[W1_ROWS:, :].bitcast(I32), 0)
         nc.vector.memset(w1s[:].rearrange("p e c -> p (e c)").bitcast(I32), 0)
-        nc.gpsimd.memset(window_s[:], 0.0)
+        nc.gpsimd.memset(window_v[:], 0.0)
+        nc.gpsimd.memset(window_s[:, :SEED], 0.0)
 
         def load_x_scales(queue, q):
             rows = x_scales[0, ROWS * q : ROWS * (q + 1), :].bitcast(I32)
@@ -94,7 +97,7 @@ def tile_moe_res_mlp_silu_kernel(
             load_x_scales(nc.sync if q < 2 else nc.scalar, q)
         load_w1_words(0, nc.sync)
         nc.sync.dma_start(xw[:], x_words[0].rearrange("p t r -> p (t r)").bitcast(I32))
-        nc.scalar.activation(warm[:, 0:1], window_s[:, 0:1], SILU)
+        nc.scalar.activation(warm[:, 0:1], window_v[:, 0:1], SILU)
         for q in range(QUADS):
             queue = nc.sync if q < 2 else nc.scalar
             queue.dma_start(
@@ -113,8 +116,6 @@ def tile_moe_res_mlp_silu_kernel(
             )
 
         regroup_w1(0, nc.scalar.copy)
-        window_v = reused.tile([P, T], F32, name="window_v", align_bytes=64, offset=0)
-        nc.gpsimd.memset(window_v[:], 0.0)
         nc.sync.dma_start(w2w[:].bitcast(I32), w2_words.rearrange("e o p c -> p (e o) c").bitcast(I32))
         for q in range(QUADS):
             queue = nc.sync if q < 2 else nc.scalar
@@ -126,6 +127,10 @@ def tile_moe_res_mlp_silu_kernel(
         nc.sync.dma_start(gate_first[:], gate[:, : 2 * C])
         gate_rest = reused.tile([P, 2 * C], F32, name="gate_rest", align_bytes=64, offset=16448)
         nc.sync.dma_start(gate_rest[:], gate[:, 2 * C :])
+        nc.sync.dma_start(
+            window_s[:, SEED:].rearrange("p (r c) -> p r c", c=SEED),
+            window_s[:, :SEED].unsqueeze(1).to_broadcast([P, T // SEED - 1, SEED]),
+        )
 
         def entries(first, last):
             return offsets[:, first // 16 : last // 16]

@@ -29,10 +29,11 @@ WORD_CUTS = (0, 160, 320, 512, 768, 1024)
 W1_LOADS = ((0, 1), (1, 2), (2, 4))
 A_BANK = (0, 1, 2, 3, 4, 5, 3, 4)
 Y_BANK = (0, 1, 4, 2)
-VECTOR_PIECES = ((0, 160), (832, 1024))
-SCALAR_PIECES = ((160, 512), (512, 832))
+VECTOR_PIECES = ((0, 160), (512, 704))
+SCALAR_PIECES = ((160, 512), (704, 1024))
 HW_AT = {}
 SEED = 256
+GPSIMD_ZEROES = 640
 OUT_PIECES = (160,) * 8
 
 
@@ -67,8 +68,9 @@ def tile_moe_res_mlp_silu_kernel(
 
         nc.vector.memset(w1s_rows[W1_ROWS:, :].bitcast(I32), 0)
         nc.vector.memset(w1s[:].rearrange("p e c -> p (e c)").bitcast(I32), 0)
-        nc.gpsimd.memset(window_v[:], 0.0)
-        nc.gpsimd.memset(window_s[:, :SEED], 0.0)
+        nc.gpsimd.memset(window_v[:, :GPSIMD_ZEROES], 0.0)
+        nc.vector.memset(window_s[:, :SEED], 0.0)
+        nc.vector.memset(window_v[:, GPSIMD_ZEROES:], 0.0)
 
         def load_x_scales(queue, q):
             rows = x_scales[0, ROWS * q : ROWS * (q + 1), :].bitcast(I32)
@@ -97,7 +99,7 @@ def tile_moe_res_mlp_silu_kernel(
             load_x_scales(nc.sync if q < 2 else nc.scalar, q)
         load_w1_words(0, nc.sync)
         nc.sync.dma_start(xw[:], x_words[0].rearrange("p t r -> p (t r)").bitcast(I32))
-        nc.scalar.activation(warm[:, 0:1], window_v[:, 0:1], SILU)
+        nc.scalar.activation(warm[:, 0:1], window_s[:, 0:1], SILU)
         for q in range(QUADS):
             queue = nc.sync if q < 2 else nc.scalar
             queue.dma_start(

@@ -33,7 +33,7 @@ VECTOR_PIECES = ((0, 160), (512, 704))
 SCALAR_PIECES = ((160, 512), (704, 1024))
 HW_AT = {}
 SEED = 256
-GPSIMD_ZEROES = 640
+GPSIMD_ZEROES = 960
 OUT_PIECES = (160,) * 8
 
 

@@ -24,13 +24,13 @@ QUADS = 4
 ROWS = 4
 W1_ROWS = QUADS * ROWS * E
 SLOTS = 128
-BYTE_CUTS = (0, 256, 640, 1024)
+BYTE_CUTS = (0, 256, 768, 1024)
 WORD_CUTS = (0, 160, 320, 512, 768, 1024)
 W1_LOADS = ((0, 1), (1, 2), (2, 4))
 A_BANK = (0, 1, 2, 3, 4, 5, 3, 4)
 Y_BANK = (0, 1, 4, 2)
-VECTOR_PIECES = ((0, 160), (512, 704))
-SCALAR_PIECES = ((160, 512), (704, 1024))
+VECTOR_PIECES = ((0, 160), (512, 736))
+SCALAR_PIECES = ((160, 512), (736, 1024))
 HW_AT = {}
 SEED = 256
 GPSIMD_ZEROES = 960

@@ -34,7 +34,9 @@ SCALAR_PIECES = ((160, 512), (736, 1024))
 HW_AT = {}
 SEED = 256
 GPSIMD_ZEROES = 960
-OUT_PIECES = (160,) * 8
+OUT_WIDTH = 160
+EARLY_PIECES = 6
+LEAD = 2
 
 
 def tile_moe_res_mlp_silu_kernel(
@@ -245,15 +247,18 @@ def tile_moe_res_mlp_silu_kernel(
         scatter_on_vector(1)
         for first, last in SCALAR_PIECES:
             nc.scalar.activation(window_s[:].indirect(entries(first, last)), gated[:, first:last], COPY)
-        for half in range(2):
-            cols = slice(half * T // 2, (half + 1) * T // 2)
-            nc.vector.tensor_tensor(partial[:, cols], window_v[:, cols], resid[:, cols], ADD)
 
-        c0 = 0
-        for piece, width in enumerate(OUT_PIECES):
-            cols = slice(c0, c0 + width)
-            total = keep.tile([P, width], F32, name=f"total{piece}")
+        def add_residual(first, last):
+            nc.vector.tensor_tensor(partial[:, first:last], window_v[:, first:last], resid[:, first:last], ADD)
+
+        add_residual(0, EARLY_PIECES * OUT_WIDTH // 2)
+        add_residual(EARLY_PIECES * OUT_WIDTH // 2, EARLY_PIECES * OUT_WIDTH)
+        for piece in range(T // OUT_WIDTH):
+            cols = slice(piece * OUT_WIDTH, (piece + 1) * OUT_WIDTH)
+            total = keep.tile([P, OUT_WIDTH], F32, name=f"total{piece}")
             nc.vector.tensor_tensor(total[:], window_s[:, cols], partial[:, cols], ADD)
             queue = nc.sync if piece % 2 == 0 else nc.scalar
             queue.dma_start(out[:, cols], total[:])
-            c0 += width
+            ahead = piece + LEAD
+            if EARLY_PIECES <= ahead < T // OUT_WIDTH:
+                add_residual(ahead * OUT_WIDTH, (ahead + 1) * OUT_WIDTH)

from contextlib import ExitStack

import concourse.mybir as mybir

K, T, E, C, H, N = 512, 1280, 4, 256, 512, 128
FLOPS = 2 * E * C * (K * H + H * N)

F32 = mybir.dt.float32
BF16 = mybir.dt.bfloat16
I32 = mybir.dt.int32
U32 = mybir.dt.uint32
U16 = mybir.dt.uint16
U8 = mybir.dt.uint8
FP8X4 = mybir.dt.float8_e4m3fn_x4
FP4X4 = mybir.dt.float4_e2m1fn_x4
SILU = mybir.ActivationFunctionType.Silu
COPY = mybir.ActivationFunctionType.Copy
MULT = mybir.AluOpType.mult
ADD = mybir.AluOpType.add

P = 128
PACK = 4
QUADS = 4
ROWS = 4
W1_ROWS = QUADS * ROWS * E
SLOTS = 128
BYTE_CUTS = (0, 256, 768, 1024)
WORD_CUTS = (0, 160, 320, 512, 768, 1024)
W1_LOADS = ((0, 1), (1, 2), (2, 4))
A_BANK = (0, 1, 2, 3, 4, 5, 3, 4)
Y_BANK = (0, 1, 4, 2)
VECTOR_PIECES = ((0, 160), (512, 736))
SCALAR_PIECES = ((160, 512), (736, 1024))
HW_AT = {}
SEED = 256
GPSIMD_ZEROES = 960
OUT_WIDTH = 160
EARLY_PIECES = 6
LEAD = 2


def tile_moe_res_mlp_silu_kernel(
    tc, x_words, x_scales, xr, w1_words, w1_scales, w2_words, w2_scales, gate, offs, out
):
    nc = tc.nc
    with ExitStack() as ctx:
        keep = ctx.enter_context(tc.tile_pool(name="keep", bufs=1))
        psum = ctx.enter_context(tc.psum_pool(name="psum", bufs=1))
        reused = ctx.enter_context(tc.tile_pool(name="reused", bufs=1))
        banks = [psum.tile([P, PACK * SLOTS], F32, name=f"bank{b}") for b in range(6)]
        offsets = keep.tile([P, E * C // 16], U16, name="offsets")
        xw = reused.tile([P, T], I32, name="xw", align_bytes=64, offset=8192)
        xs = keep.tile([P, T], U8, name="xs", align_bytes=64)
        w1w = [
            reused.tile([P, 1, 2 * H], U8, name="w1w0", align_bytes=64, offset=0),
            reused.tile([P, 1, 2 * H], U8, name="w1w1", align_bytes=64, offset=16384),
            reused.tile([P, 2, 2 * H], U8, name="w1w2", align_bytes=64, offset=20480),
        ]
        w1s_rows = keep.tile([P, H], U8, name="w1s_rows", align_bytes=64)
        w1s_regrouped = reused.tile([P, H], U8, name="w1s_regrouped", align_bytes=64, offset=4 * T)
        w1s = keep.tile([P, E, H], U8, name="w1s", align_bytes=64)
        w2w = keep.tile([P, E, 2 * N], U8, name="w2w", align_bytes=64)
        w2s = w1s_rows[:].rearrange("p (e c) -> p e c", e=E)
        gate_first = keep.tile([P, 2 * C], F32, name="gate_first")
        window_s = keep.tile([P, T], F32, name="window_s")
        window_v = keep.tile([P, T], F32, name="window_v")
        partial = keep.tile([P, T], F32, name="partial")
        gated = keep.tile([P, E * C], F32, name="gated")
        warm = keep.tile([P, 8], F32, name="warm")

        nc.vector.memset(w1s_rows[W1_ROWS:, :].bitcast(I32), 0)
        nc.vector.memset(w1s[:].rearrange("p e c -> p (e c)").bitcast(I32), 0)
        nc.gpsimd.memset(window_v[:, :GPSIMD_ZEROES], 0.0)
        nc.vector.memset(window_s[:, :SEED], 0.0)
        nc.vector.memset(window_v[:, GPSIMD_ZEROES:], 0.0)

        def load_x_scales(queue, q):
            rows = x_scales[0, ROWS * q : ROWS * (q + 1), :].bitcast(I32)
            queue.dma_start(
                xs[32 * q : 32 * (q + 1), :].bitcast(I32),
                rows.unsqueeze(0).to_broadcast([32 // ROWS, ROWS, T // 4]),
            )

        def load_w1_words(h, queue):
            words = w1_words.rearrange("e o p c -> p (e o) c").bitcast(I32)
            queue.dma_start(w1w[h][:].bitcast(I32), words[:, W1_LOADS[h][0] : W1_LOADS[h][1], :])

        def raw_w1(e):
            h = max(i for i, (first, last) in enumerate(W1_LOADS) if first <= e)
            return w1w[h][:, e - W1_LOADS[h][0], :]

        nc.sync.dma_start(offsets[:], offs)
        nc.scalar.dma_start(
            w1s_rows[:W1_ROWS, :].bitcast(I32), w1_scales[:, 0, :, :].rearrange("e f c -> f e c").bitcast(I32)
        )
        nc.vector.tensor_copy(
            w1s_regrouped[:].rearrange("r (t m) -> r t m", t=PACK),
            w1s_rows[:].rearrange("r (m t) -> r t m", t=PACK),
        )
        for q in range(QUADS):
            load_x_scales(nc.sync if q < 2 else nc.scalar, q)
        load_w1_words(0, nc.sync)
        nc.sync.dma_start(xw[:], x_words[0].rearrange("p t r -> p (t r)").bitcast(I32))
        nc.scalar.activation(warm[:, 0:1], window_s[:, 0:1], SILU)
        for q in range(QUADS):
            queue = nc.sync if q < 2 else nc.scalar
            queue.dma_start(
                w1s[32 * q : 32 * q + ROWS, :, :].bitcast(I32),
                w1s_regrouped[ROWS * E * q : ROWS * E * (q + 1), :].bitcast(I32),
            )
        load_w1_words(1, nc.sync)
        load_w1_words(2, nc.sync)
        w1g = {}

        def regroup_w1(e, regroup):
            w1g[e] = keep.tile([P, 2 * H], U8, name=f"w1g{e}", align_bytes=64)
            regroup(
                w1g[e][:].bitcast(U16).rearrange("p (t m) -> p t m", t=PACK),
                raw_w1(e).bitcast(U16).rearrange("p (m t) -> p t m", t=PACK),
            )

        regroup_w1(0, nc.scalar.copy)
        nc.sync.dma_start(w2w[:].bitcast(I32), w2_words.rearrange("e o p c -> p (e o) c").bitcast(I32))
        for q in range(QUADS):
            queue = nc.sync if q < 2 else nc.scalar
            queue.dma_start(
                w2s[32 * q : 32 * q + ROWS, :, :].bitcast(I32),
                w2_scales[:, 0, ROWS * q : ROWS * (q + 1), :].rearrange("e j c -> j e c").bitcast(I32),
            )
        regroup_w1(1, nc.scalar.copy)
        nc.sync.dma_start(gate_first[:], gate[:, : 2 * C])
        gate_rest = reused.tile([P, 2 * C], F32, name="gate_rest", align_bytes=64, offset=16448)
        nc.sync.dma_start(gate_rest[:], gate[:, 2 * C :])
        nc.sync.dma_start(
            window_s[:, SEED:].rearrange("p (r c) -> p r c", c=SEED),
            window_s[:, :SEED].unsqueeze(1).to_broadcast([P, T // SEED - 1, SEED]),
        )

        def entries(first, last):
            return offsets[:, first // 16 : last // 16]

        gs_first = keep.tile([P, BYTE_CUTS[2]], U8, name="gs_first", align_bytes=64)
        gs_last = reused.tile([P, E * C - BYTE_CUTS[2]], U8, name="gs_last", align_bytes=64, offset=4 * T)

        def gs(first, last):
            cut = BYTE_CUTS[2]
            return gs_first[:, first:last] if first < cut else gs_last[:, first - cut : last - cut]

        gw = keep.tile([P, E * C], U32, name="gw", align_bytes=64)

        def gather_bytes(i):
            first, last = BYTE_CUTS[i], BYTE_CUTS[i + 1]
            nc.vector.tensor_copy(gs(first, last), xs[:].indirect(entries(first, last)))

        def gather_words(i):
            first, last = WORD_CUTS[i], WORD_CUTS[i + 1]
            nc.vector.tensor_copy(gw[:, first:last], xw[:].bitcast(U32).indirect(entries(first, last)))

        gather_bytes(0)
        gather_bytes(1)
        gather_words(0)
        gather_words(1)
        gather_words(2)
        gather_bytes(2)
        gather_words(3)
        gather_words(4)
        resid = reused.tile([P, T], F32, name="resid", align_bytes=64, offset=8192)
        nc.sync.dma_start(resid[:], xr)
        regroup_w1(2, nc.vector.tensor_copy)
        regroup_w1(3, nc.vector.tensor_copy)

        hb = {}

        def first_layer(e):
            if e == 0:
                hb[e] = reused.tile([P, C, PACK], BF16, name=f"hb{e}", align_bytes=64, offset=14400)
            else:
                hb[e] = keep.tile([P, C, PACK], BF16, name=f"hb{e}", align_bytes=64)
            for half in range(C // SLOTS):
                b = e * C // SLOTS + half
                cols = slice(b * SLOTS, (b + 1) * SLOTS)
                a = banks[A_BANK[b]][:].rearrange("p (t s) -> p t s", t=PACK)
                for t in range(PACK):
                    nc.tensor.matmul_mx(
                        out=a[:, t, :],
                        lhsT=w1g[e][:, 2 * P * t : 2 * P * (t + 1)].bitcast(FP4X4),
                        lhsT_scale=w1s[:, e, P * t : P * (t + 1)],
                        rhs=gw[:, cols].bitcast(FP8X4),
                        rhs_scale=gs(b * SLOTS, (b + 1) * SLOTS),
                        start=True,
                        stop=True,
                    )
                nc.scalar.activation(
                    hb[e][:, half * SLOTS : (half + 1) * SLOTS, :], a.rearrange("p t s -> p s t"), SILU
                )

        codes = {}

        def quantise(e):
            if e in HW_AT:
                hw = reused.tile([P, C], U32, name=f"hw{e}", align_bytes=64, offset=HW_AT[e])
            else:
                hw = keep.tile([P, C], U32, name=f"hw{e}", align_bytes=64)
            hs = keep.tile([P, C], U8, name=f"hs{e}", align_bytes=64)
            nc.vector.quantize_mx(
                out=hw[:].bitcast(FP8X4), scales=hs[:], in_=hb[e][:].rearrange("p s t -> p (s t)")
            )
            codes[e] = hw, hs

        def second_layer(e):
            hw, hs = codes[e]
            y = banks[Y_BANK[e]][:, :C]
            nc.tensor.matmul_mx(
                out=y,
                lhsT=w2w[:, e, :].bitcast(FP4X4),
                lhsT_scale=w2s[:, e, :],
                rhs=hw[:].bitcast(FP8X4),
                rhs_scale=hs[:],
                start=True,
                stop=True,
            )

        def gate_product(e):
            cols = slice(e * C, (e + 1) * C)
            nc.vector.tensor_tensor(gated[:, cols], banks[Y_BANK[e]][:, :C], (gate_first if e < 2 else gate_rest)[:, e % 2 * C : (e % 2 + 1) * C], MULT)

        def scatter_on_vector(i):
            first, last = VECTOR_PIECES[i]
            nc.vector.tensor_copy(window_v[:].indirect(entries(first, last)), gated[:, first:last])

        for e in range(E - 1):
            first_layer(e)
        quantise(0)
        second_layer(0)
        gate_product(0)
        quantise(1)
        second_layer(1)
        first_layer(E - 1)
        scatter_on_vector(0)
        gate_product(1)
        quantise(2)
        quantise(3)
        second_layer(2)
        gate_product(2)
        second_layer(3)
        gate_product(3)
        scatter_on_vector(1)
        for first, last in SCALAR_PIECES:
            nc.scalar.activation(window_s[:].indirect(entries(first, last)), gated[:, first:last], COPY)

        def add_residual(first, last):
            nc.vector.tensor_tensor(partial[:, first:last], window_v[:, first:last], resid[:, first:last], ADD)

        add_residual(0, EARLY_PIECES * OUT_WIDTH // 2)
        add_residual(EARLY_PIECES * OUT_WIDTH // 2, EARLY_PIECES * OUT_WIDTH)
        for piece in range(T // OUT_WIDTH):
            cols = slice(piece * OUT_WIDTH, (piece + 1) * OUT_WIDTH)
            total = keep.tile([P, OUT_WIDTH], F32, name=f"total{piece}")
            nc.vector.tensor_tensor(total[:], window_s[:, cols], partial[:, cols], ADD)
            queue = nc.sync if piece % 2 == 0 else nc.scalar
            queue.dma_start(out[:, cols], total[:])
            ahead = piece + LEAD
            if EARLY_PIECES <= ahead < T // OUT_WIDTH:
                add_residual(ahead * OUT_WIDTH, (ahead + 1) * OUT_WIDTH)
